import numpy as np
import ml_dtypes


def mxq(x, axis, fmt="e4m3"):
    dtype, down = {"e4m3": (ml_dtypes.float8_e4m3fn, 7), "e5m2": (ml_dtypes.float8_e5m2, 14)}[fmt]
    v = np.moveaxis(np.asarray(x, np.float32).astype(ml_dtypes.bfloat16).astype(np.float64), axis, -1)
    blocks = v.reshape(v.shape[:-1] + (-1, 32))
    amax = np.abs(blocks).max(-1, keepdims=True)
    byte = np.maximum(np.where(amax > 0, np.frexp(amax)[1] - 1 + 127, 0) - down, 1)
    scale = np.exp2(byte - 127.0)
    codes = (blocks / scale).astype(np.float32).astype(dtype).astype(np.float64)
    return np.moveaxis((codes * scale).reshape(v.shape), -1, axis)


WIDE = False


def mx_kscale(k):
    if not WIDE:
        return np.ones(k)
    levels = np.array([10, -10, 5, -5, 0])
    if k % 512:
        return np.exp2(np.random.permutation(np.resize(levels, k // 32))).repeat(32)
    a = np.empty((k // 512, 16))
    for p in range(k // 512):
        a[p, :8] = np.random.permutation(np.resize(levels, 8))
        for g in range(8):
            far = levels[np.abs(levels - a[p, g]) >= 10]
            a[p, g + 8] = far[np.random.randint(len(far))]
    return np.exp2(a.ravel()).repeat(32)


def f64(x):
    return np.asarray(x).astype(np.float64)


def striped(idx):
    return np.tile(idx.reshape(-1, 16).T, (8, 1)).astype(np.uint16)


def unstriped(offs):
    return offs[:16].T.reshape(-1).astype(np.int64)


def pack_weight(w):
    k, n = w.shape
    w = f64(np.asarray(w, np.float32).astype(ml_dtypes.bfloat16)).reshape(k // 32, 32, n)
    amax = np.abs(w).max(1)
    byte = np.clip(np.where(amax > 0, np.frexp(amax)[1] - 1 + 127 - 7, 1), 1, 254)
    scaled = (w * np.exp2(127.0 - byte)[:, None, :]).reshape(k, n).astype(np.float32)
    words = np.ascontiguousarray(scaled.reshape(k // 512, 128, 4, n).transpose(0, 1, 3, 2)).astype(ml_dtypes.float8_e4m3fn).view(np.uint8)
    return words, np.ascontiguousarray(byte.astype(np.uint8).reshape(k // 512, 16, n))


def unpack_weight(words, scales):
    g, p, n, _ = words.shape
    vals = np.ascontiguousarray(words).view(ml_dtypes.float8_e4m3fn).astype(np.float64) * np.repeat(np.exp2(scales.astype(np.float64) - 127.0), 8, axis=1)[..., None]
    return vals.transpose(0, 1, 3, 2).reshape(g * 512, n)

def planes(y):
    n, m = y.shape
    v = y.astype(np.float32).astype(ml_dtypes.bfloat16).astype(np.float64).reshape(n // 32, 32, m)
    top = np.abs(v).max(1)
    byte = np.clip(np.where(top > 0, np.frexp(top)[1] - 1 + 127 - 7, 1), 1, 254)
    codes = (v * np.exp2(127.0 - byte)[:, None, :]).reshape(n, m).astype(np.float32).astype(ml_dtypes.float8_e4m3fn).view(np.uint8)
    words = codes.reshape(n // 512, 128, 4, m).transpose(0, 1, 3, 2)
    return np.ascontiguousarray(words), np.ascontiguousarray(byte.astype(np.uint8).reshape(n // 512, 16, m))


K, T, S, N = 512, 1024, 512, 512
P = 2 ** 7


def setup_inputs():
    n = np.random.standard_normal
    s = mx_kscale(K)[:, None]
    packed_xT = pack_weight(n((K, T)) * s)
    return {
        "x_words": packed_xT[0],
        "x_scales": packed_xT[1],
        "tscale": np.tile(np.random.uniform(0.25, 2.0, T), (P, 1)).astype(np.float32),
        "cscale": np.random.uniform(0.5, 1.5, (N, 1)).astype(np.float32),
        "w1": (n((K, N)) / np.sqrt(K) / s).astype(np.float32),
        "offs": striped(np.random.permutation(T)[:S]),
    }


def reference(x_words, x_scales, tscale, cscale, w1, offs):
    xq = unpack_weight(x_words, x_scales)[:, unstriped(offs)]
    y = mxq(f64(w1), 0, "e4m3").T @ xq
    tg = f64(tscale)[:1][:, unstriped(offs)]
    out_0 = (f64(cscale) * y) * tg
    return (out_0,) + planes(out_0)

@@ -1,0 +1,167 @@
+from contextlib import ExitStack
+
+import concourse.mybir as mybir
+from concourse.masks import make_identity
+
+K, T, S, N = 512, 1024, 512, 512
+FLOPS = 2 * K * S * N
+
+F32 = mybir.dt.float32
+BF16 = mybir.dt.bfloat16
+I32 = mybir.dt.int32
+U32 = mybir.dt.uint32
+U16 = mybir.dt.uint16
+U8 = mybir.dt.uint8
+FP8X4 = mybir.dt.float8_e4m3fn_x4
+MULT = mybir.AluOpType.mult
+
+P = 128
+PACK = 4
+W_HALF = N // 2
+CHUNK = 128
+
+
+def tile_picked_tokscale_none_po_kernel(tc, x_words, x_scales, tscale, cscale, w1, offs, out_0, out_1, out_2):
+    nc = tc.nc
+    with ExitStack() as ctx:
+        keep = ctx.enter_context(tc.tile_pool(name="keep", bufs=1))
+        psum = ctx.enter_context(tc.psum_pool(name="psum", bufs=1))
+
+        offsets = keep.tile([P, S // 16], U16, name="offsets")
+        nc.sync.dma_start(offsets[:], offs)
+
+        ts_rows = keep.tile([P, T // P], F32, name="ts_rows", tag="rows_then_w", align_bytes=64)
+        nc.scalar.dma_start(ts_rows[:], tscale[0].rearrange("(n c) -> n c", c=T // P))
+
+        xs_window = keep.tile([P, T], U8, name="xs_window", tag="bytes_then_words", align_bytes=64)
+        for q in range(4):
+            rows = x_scales[0, 4 * q : 4 * q + 4, :].bitcast(I32)
+            engine = nc.sync if q % 2 == 0 else nc.scalar
+            engine.dma_start(
+                xs_window[32 * q : 32 * q + 32, :].bitcast(I32),
+                rows.unsqueeze(0).to_broadcast([8, 4, T // 4]),
+            )
+
+        xw_window = keep.tile([P, T], I32, name="xw_window", align_bytes=64)
+        nc.sync.dma_start(xw_window[:], x_words[0].rearrange("p n t -> p (n t)").bitcast(I32))
+
+        w_view = w1.rearrange("(p j) m -> p j m", j=PACK)
+        w_raw = []
+        for h in range(2):
+            raw = keep.tile([P, PACK, W_HALF], F32, name="w_raw%d" % h, tag="w_raw%d" % h, align_bytes=64)
+            nc.sync.dma_start(raw[:], w_view[:, :, h * W_HALF : (h + 1) * W_HALF])
+            w_raw.append(raw)
+
+        cs = keep.tile([P, PACK], F32, name="cs")
+        nc.sync.dma_start(cs[:], cscale.rearrange("(p t) o -> p (t o)", t=PACK))
+
+        ident = keep.tile([P, P], F32, name="ident")
+        make_identity(nc, ident[:])
+
+        ts_window = keep.tile([P, T], F32, name="ts_window", align_bytes=64)
+        ts_view = ts_window[:].rearrange("p (n c) -> p n c", c=T // P)
+        for b in range(2):
+            spread = psum.tile([P, 4, P], F32, name="spread%d" % b, tag="bank%d" % b)
+            for c in range(4):
+                col = 4 * b + c
+                nc.tensor.transpose(spread[:, c, :], ts_rows[:, col : col + 1].to_broadcast([P, P]), ident[:])
+            nc.scalar.copy(ts_view[:, :, 4 * b : 4 * b + 4], spread[:].rearrange("p c n -> p n c"))
+
+        xs_picked = keep.tile([P, S], U8, name="xs_picked", align_bytes=64)
+        nc.vector.tensor_copy(xs_picked[:], xs_window[:].indirect(offsets[:]))
+
+        w_codes = keep.tile([P, N], U32, name="w_codes", align_bytes=64)
+        w_scales = keep.tile([P, N], U8, name="w_scales", align_bytes=64)
+        half_m = W_HALF // PACK
+        w_bf = []
+        for h in range(2):
+            tag = "rows_then_w" if h == 0 else "w_raw0"
+            bf = keep.tile([P, W_HALF * PACK], BF16, name="w_bf%d" % h, tag=tag, align_bytes=64)
+            w_bf.append(bf)
+
+        def round_w(copy, h, m0, m1):
+            copy(
+                w_bf[h][:].rearrange("p (t m j) -> p m j t", t=PACK, j=PACK)[:, m0:m1],
+                w_raw[h][:].rearrange("p j (m t) -> p m j t", t=PACK)[:, m0:m1],
+            )
+
+        round_w(nc.scalar.copy, 0, 0, half_m)
+        round_w(nc.scalar.copy, 1, 0, half_m // 2)
+
+        n_chunks = S // CHUNK
+        xw_picked = keep.tile([P, S], U32, name="xw_picked", tag="bytes_then_words", align_bytes=64)
+        nc.vector.tensor_copy(xw_picked[:], xw_window[:].bitcast(U32).indirect(offsets[:]))
+        ts_picked = []
+
+        def pick_ts(half, tag):
+            tile = keep.tile([P, S // 2], F32, name="ts_picked%d" % half, tag=tag, align_bytes=64)
+            nc.vector.tensor_copy(tile[:], ts_window[:].indirect(offsets[:, half * S // 32 : (half + 1) * S // 32]))
+            ts_picked.append(tile)
+
+        pick_ts(0, "ts_picked0")
+        round_w(nc.vector.tensor_copy, 1, half_m // 2, half_m)
+        for h in range(2):
+            for t in range(PACK):
+                cols = slice(t * P + h * half_m, t * P + (h + 1) * half_m)
+                nc.vector.quantize_mx(
+                    out=w_codes[:, cols].bitcast(FP8X4),
+                    scales=w_scales[:, cols],
+                    in_=w_bf[h][:, t * W_HALF : (t + 1) * W_HALF],
+                )
+        pick_ts(1, "w_raw0")
+
+        y_codes = keep.tile([P, S], I32, name="y_codes", align_bytes=64)
+        y_scales = keep.tile([P, S], U8, name="y_scales", align_bytes=64)
+        y_bf = keep.tile([P, S * PACK], BF16, name="y_bf", align_bytes=64)
+        out_rows = out_0.rearrange("(p t) s -> p t s", t=PACK)
+        out_words = out_1[0].rearrange("p s t -> p (s t)").bitcast(I32)
+        y = []
+
+        def round_y(copy, c, s0, s1):
+            copy(
+                y_bf[:, (c * CHUNK + s0) * PACK : (c * CHUNK + s1) * PACK].rearrange("p (g i t) -> p g t i", i=4, t=PACK),
+                y[c][:, :, s0:s1].rearrange("p t (g i) -> p g t i", i=4),
+            )
+
+        def quantize_y(s0, s1):
+            nc.vector.quantize_mx(
+                out=y_codes[:, s0:s1].bitcast(FP8X4), scales=y_scales[:, s0:s1], in_=y_bf[:, s0 * PACK : s1 * PACK]
+            )
+
+        for c in range(n_chunks):
+            cols = slice(c * CHUNK, (c + 1) * CHUNK)
+            acc = [
+                psum.tile([P, CHUNK], F32, name="acc%d_%d" % (c, t), tag="bank%d" % (c % 2 * PACK + t))[:]
+                for t in range(PACK)
+            ]
+            ts_cols = ts_picked[c // 2][:, c % 2 * CHUNK : (c % 2 + 1) * CHUNK]
+            for t in range(PACK):
+                nc.tensor.matmul_mx(
+                    out=acc[t],
+                    lhsT=w_codes[:, t * P : (t + 1) * P].bitcast(FP8X4),
+                    lhsT_scale=w_scales[:, t * P : (t + 1) * P],
+                    rhs=xw_picked[:, cols].bitcast(FP8X4),
+                    rhs_scale=xs_picked[:, cols],
+                    start=True,
+                    stop=True,
+                )
+            tile = keep.tile([P, PACK, CHUNK], F32, name="y%d" % c, align_bytes=64)
+            y.append(tile)
+            for t in range(PACK):
+                nc.vector.scalar_tensor_tensor(tile[:, t, :], acc[t], cs[:, t : t + 1], ts_cols, MULT, MULT)
+            nc.sync.dma_start(out_rows[:, :, cols], tile[:])
+            round_y(nc.scalar.copy, c, 0, CHUNK if c < n_chunks - 1 else CHUNK // 2)
+
+        quantize_y(0, 2 * CHUNK)
+        nc.sync.dma_start(out_words[:, : 2 * CHUNK], y_codes[:, : 2 * CHUNK])
+        round_y(nc.vector.tensor_copy, n_chunks - 1, CHUNK // 2, CHUNK)
+        quantize_y(2 * CHUNK, 3 * CHUNK)
+        quantize_y(3 * CHUNK, S)
+        nc.sync.dma_start(out_words[:, 2 * CHUNK :], y_codes[:, 2 * CHUNK :])
+
+        for q in range(4):
+            engine = nc.sync if q < 2 else nc.scalar
+            engine.dma_start(
+                out_2[0, 4 * q : 4 * q + 4, :].bitcast(I32),
+                y_scales[32 * q : 32 * q + 4, :].bitcast(I32),
+            )

@@ -1,7 +1,6 @@
 from contextlib import ExitStack
 
 import concourse.mybir as mybir
-from concourse.masks import make_identity
 
 K, T, S, N = 512, 1024, 512, 512
 FLOPS = 2 * K * S * N
@@ -14,6 +13,8 @@ U16 = mybir.dt.uint16
 U8 = mybir.dt.uint8
 FP8X4 = mybir.dt.float8_e4m3fn_x4
 MULT = mybir.AluOpType.mult
+ADD = mybir.AluOpType.add
+IS_EQUAL = mybir.AluOpType.is_equal
 
 P = 128
 PACK = 4
@@ -55,8 +56,17 @@ def tile_picked_tokscale_none_po_kernel(tc, x_words, x_scales, tscale, cscale, w
         cs = keep.tile([P, PACK], F32, name="cs")
         nc.sync.dma_start(cs[:], cscale.rearrange("(p t) o -> p (t o)", t=PACK))
 
+        ones = keep.tile([P, 32], F32, name="ones")
+        nc.vector.memset(ones[:], 1.0)
         ident = keep.tile([P, P], F32, name="ident")
-        make_identity(nc, ident[:])
+        nc.vector.memset(ident[:], 0.0)
+        column_count = keep.tile([P, 32], F32, name="column_count", align_bytes=64)
+        nc.vector.tensor_tensor_scan(column_count[:], ones[:], ones[:], 0.0, MULT, ADD)
+        row_count = keep.tile([P, 32], F32, name="row_count", align_bytes=64)
+        nc.vector.transpose(row_count[:], column_count[:])
+        for q in range(4):
+            block = slice(32 * q, 32 * q + 32)
+            nc.vector.tensor_tensor(ident[block, block], column_count[block, :], row_count[block, :], IS_EQUAL)
 
         ts_window = keep.tile([P, T], F32, name="ts_window", align_bytes=64)
         ts_view = ts_window[:].rearrange("p (n c) -> p n c", c=T // P)
@@ -93,12 +103,12 @@ def tile_picked_tokscale_none_po_kernel(tc, x_words, x_scales, tscale, cscale, w
         nc.vector.tensor_copy(xw_picked[:], xw_window[:].bitcast(U32).indirect(offsets[:]))
         ts_picked = []
 
-        def pick_ts(half, tag):
-            tile = keep.tile([P, S // 2], F32, name="ts_picked%d" % half, tag=tag, align_bytes=64)
-            nc.vector.tensor_copy(tile[:], ts_window[:].indirect(offsets[:, half * S // 32 : (half + 1) * S // 32]))
-            ts_picked.append(tile)
+        def pick_ts(c0, c1, tag):
+            tile = keep.tile([P, (c1 - c0) * CHUNK], F32, name="ts_picked%d" % c0, tag=tag, align_bytes=64)
+            nc.vector.tensor_copy(tile[:], ts_window[:].indirect(offsets[:, c0 * CHUNK // 16 : c1 * CHUNK // 16]))
+            ts_picked.extend(tile[:, i * CHUNK : (i + 1) * CHUNK] for i in range(c1 - c0))
 
-        pick_ts(0, "ts_picked0")
+        pick_ts(0, n_chunks - 1, "ts_picked0")
         round_w(nc.vector.tensor_copy, 1, half_m // 2, half_m)
         for h in range(2):
             for t in range(PACK):
@@ -108,7 +118,7 @@ def tile_picked_tokscale_none_po_kernel(tc, x_words, x_scales, tscale, cscale, w
                     scales=w_scales[:, cols],
                     in_=w_bf[h][:, t * W_HALF : (t + 1) * W_HALF],
                 )
-        pick_ts(1, "w_raw0")
+        pick_ts(n_chunks - 1, n_chunks, "w_raw0")
 
         y_codes = keep.tile([P, S], I32, name="y_codes", align_bytes=64)
         y_scales = keep.tile([P, S], U8, name="y_scales", align_bytes=64)
@@ -134,7 +144,6 @@ def tile_picked_tokscale_none_po_kernel(tc, x_words, x_scales, tscale, cscale, w
                 psum.tile([P, CHUNK], F32, name="acc%d_%d" % (c, t), tag="bank%d" % (c % 2 * PACK + t))[:]
                 for t in range(PACK)
             ]
-            ts_cols = ts_picked[c // 2][:, c % 2 * CHUNK : (c % 2 + 1) * CHUNK]
             for t in range(PACK):
                 nc.tensor.matmul_mx(
                     out=acc[t],
@@ -148,7 +157,7 @@ def tile_picked_tokscale_none_po_kernel(tc, x_words, x_scales, tscale, cscale, w
             tile = keep.tile([P, PACK, CHUNK], F32, name="y%d" % c, align_bytes=64)
             y.append(tile)
             for t in range(PACK):
-                nc.vector.scalar_tensor_tensor(tile[:, t, :], acc[t], cs[:, t : t + 1], ts_cols, MULT, MULT)
+                nc.vector.scalar_tensor_tensor(tile[:, t, :], acc[t], cs[:, t : t + 1], ts_picked[c], MULT, MULT)
             nc.sync.dma_start(out_rows[:, :, cols], tile[:])
             round_y(nc.scalar.copy, c, 0, CHUNK if c < n_chunks - 1 else CHUNK // 2)
 

@@ -19,7 +19,8 @@ IS_EQUAL = mybir.AluOpType.is_equal
 P = 128
 PACK = 4
 W_HALF = N // 2
-CHUNK = 128
+CHUNK = 256
+SCALAR_LAST = 96
 
 
 def tile_picked_tokscale_none_po_kernel(tc, x_words, x_scales, tscale, cscale, w1, offs, out_0, out_1, out_2):
@@ -35,12 +36,12 @@ def tile_picked_tokscale_none_po_kernel(tc, x_words, x_scales, tscale, cscale, w
         nc.scalar.dma_start(ts_rows[:], tscale[0].rearrange("(n c) -> n c", c=T // P))
 
         xs_window = keep.tile([P, T], U8, name="xs_window", tag="bytes_then_words", align_bytes=64)
+        nc.vector.memset(xs_window[:].bitcast(I32), 0)
         for q in range(4):
-            rows = x_scales[0, 4 * q : 4 * q + 4, :].bitcast(I32)
             engine = nc.sync if q % 2 == 0 else nc.scalar
             engine.dma_start(
-                xs_window[32 * q : 32 * q + 32, :].bitcast(I32),
-                rows.unsqueeze(0).to_broadcast([8, 4, T // 4]),
+                xs_window[32 * q : 32 * q + 4, :].bitcast(I32),
+                x_scales[0, 4 * q : 4 * q + 4, :].bitcast(I32),
             )
 
         xw_window = keep.tile([P, T], I32, name="xw_window", align_bytes=64)
@@ -103,12 +104,12 @@ def tile_picked_tokscale_none_po_kernel(tc, x_words, x_scales, tscale, cscale, w
         nc.vector.tensor_copy(xw_picked[:], xw_window[:].bitcast(U32).indirect(offsets[:]))
         ts_picked = []
 
-        def pick_ts(c0, c1, tag):
-            tile = keep.tile([P, (c1 - c0) * CHUNK], F32, name="ts_picked%d" % c0, tag=tag, align_bytes=64)
-            nc.vector.tensor_copy(tile[:], ts_window[:].indirect(offsets[:, c0 * CHUNK // 16 : c1 * CHUNK // 16]))
-            ts_picked.extend(tile[:, i * CHUNK : (i + 1) * CHUNK] for i in range(c1 - c0))
+        def pick_ts(c, tag):
+            tile = keep.tile([P, CHUNK], F32, name="ts_picked%d" % c, tag=tag, align_bytes=64)
+            nc.vector.tensor_copy(tile[:], ts_window[:].indirect(offsets[:, c * CHUNK // 16 : (c + 1) * CHUNK // 16]))
+            ts_picked.append(tile)
 
-        pick_ts(0, n_chunks - 1, "ts_picked0")
+        pick_ts(0, "ts_picked0")
         round_w(nc.vector.tensor_copy, 1, half_m // 2, half_m)
         for h in range(2):
             for t in range(PACK):
@@ -118,7 +119,7 @@ def tile_picked_tokscale_none_po_kernel(tc, x_words, x_scales, tscale, cscale, w
                     scales=w_scales[:, cols],
                     in_=w_bf[h][:, t * W_HALF : (t + 1) * W_HALF],
                 )
-        pick_ts(n_chunks - 1, n_chunks, "w_raw0")
+        pick_ts(1, "w_raw0")
 
         y_codes = keep.tile([P, S], I32, name="y_codes", align_bytes=64)
         y_scales = keep.tile([P, S], U8, name="y_scales", align_bytes=64)
@@ -133,20 +134,23 @@ def tile_picked_tokscale_none_po_kernel(tc, x_words, x_scales, tscale, cscale, w
                 y[c][:, :, s0:s1].rearrange("p t (g i) -> p g t i", i=4),
             )
 
-        def quantize_y(s0, s1):
+        def quantize_y(c):
+            cols = slice(c * CHUNK, (c + 1) * CHUNK)
             nc.vector.quantize_mx(
-                out=y_codes[:, s0:s1].bitcast(FP8X4), scales=y_scales[:, s0:s1], in_=y_bf[:, s0 * PACK : s1 * PACK]
+                out=y_codes[:, cols].bitcast(FP8X4),
+                scales=y_scales[:, cols],
+                in_=y_bf[:, c * CHUNK * PACK : (c + 1) * CHUNK * PACK],
             )
+            nc.sync.dma_start(out_words[:, cols], y_codes[:, cols])
 
         for c in range(n_chunks):
             cols = slice(c * CHUNK, (c + 1) * CHUNK)
-            acc = [
-                psum.tile([P, CHUNK], F32, name="acc%d_%d" % (c, t), tag="bank%d" % (c % 2 * PACK + t))[:]
-                for t in range(PACK)
-            ]
+            tile = keep.tile([P, PACK, CHUNK], F32, name="y%d" % c, align_bytes=64)
+            y.append(tile)
             for t in range(PACK):
+                acc = psum.tile([P, CHUNK], F32, name="acc%d_%d" % (c, t), tag="bank%d" % (c * PACK + t))
                 nc.tensor.matmul_mx(
-                    out=acc[t],
+                    out=acc[:],
                     lhsT=w_codes[:, t * P : (t + 1) * P].bitcast(FP8X4),
                     lhsT_scale=w_scales[:, t * P : (t + 1) * P],
                     rhs=xw_picked[:, cols].bitcast(FP8X4),
@@ -154,22 +158,19 @@ def tile_picked_tokscale_none_po_kernel(tc, x_words, x_scales, tscale, cscale, w
                     start=True,
                     stop=True,
                 )
-            tile = keep.tile([P, PACK, CHUNK], F32, name="y%d" % c, align_bytes=64)
-            y.append(tile)
-            for t in range(PACK):
-                nc.vector.scalar_tensor_tensor(tile[:, t, :], acc[t], cs[:, t : t + 1], ts_picked[c], MULT, MULT)
-            nc.sync.dma_start(out_rows[:, :, cols], tile[:])
-            round_y(nc.scalar.copy, c, 0, CHUNK if c < n_chunks - 1 else CHUNK // 2)
+                nc.vector.scalar_tensor_tensor(tile[:, t, :], acc[:], cs[:, t : t + 1], ts_picked[c][:], MULT, MULT)
+                if c == 0 and t < 2:
+                    nc.sync.dma_start(out_rows[:, t, cols], tile[:, t, :])
+                elif t % 2 == 1:
+                    nc.sync.dma_start(out_rows[:, t - 1 : t + 1, cols], tile[:, t - 1 : t + 1, :])
+            round_y(nc.scalar.copy, c, 0, CHUNK if c == 0 else SCALAR_LAST)
 
-        quantize_y(0, 2 * CHUNK)
-        nc.sync.dma_start(out_words[:, : 2 * CHUNK], y_codes[:, : 2 * CHUNK])
-        round_y(nc.vector.tensor_copy, n_chunks - 1, CHUNK // 2, CHUNK)
-        quantize_y(2 * CHUNK, 3 * CHUNK)
-        quantize_y(3 * CHUNK, S)
-        nc.sync.dma_start(out_words[:, 2 * CHUNK :], y_codes[:, 2 * CHUNK :])
+        round_y(nc.vector.tensor_copy, 1, SCALAR_LAST, CHUNK)
+        quantize_y(0)
+        quantize_y(1)
 
         for q in range(4):
-            engine = nc.sync if q < 2 else nc.scalar
+            engine = nc.sync if q == 0 else nc.scalar
             engine.dma_start(
                 out_2[0, 4 * q : 4 * q + 4, :].bitcast(I32),
                 y_scales[32 * q : 32 * q + 4, :].bitcast(I32),

@@ -21,6 +21,7 @@ PACK = 4
 W_HALF = N // 2
 CHUNK = 256
 SCALAR_LAST = 96
+SCALAR_W = 32
 
 
 def tile_picked_tokscale_none_po_kernel(tc, x_words, x_scales, tscale, cscale, w1, offs, out_0, out_1, out_2):
@@ -35,7 +36,10 @@ def tile_picked_tokscale_none_po_kernel(tc, x_words, x_scales, tscale, cscale, w
         ts_rows = keep.tile([P, T // P], F32, name="ts_rows", tag="rows_then_w", align_bytes=64)
         nc.scalar.dma_start(ts_rows[:], tscale[0].rearrange("(n c) -> n c", c=T // P))
 
-        xs_window = keep.tile([P, T], U8, name="xs_window", tag="bytes_then_words", align_bytes=64)
+        xw_window = keep.tile([P, T], I32, name="xw_window", tag="words_then_bytes", align_bytes=64)
+        nc.sync.dma_start(xw_window[:], x_words[0].rearrange("p n t -> p (n t)").bitcast(I32))
+
+        xs_window = keep.tile([P, T], U8, name="xs_window", align_bytes=64)
         nc.vector.memset(xs_window[:].bitcast(I32), 0)
         for q in range(4):
             engine = nc.sync if q % 2 == 0 else nc.scalar
@@ -43,9 +47,6 @@ def tile_picked_tokscale_none_po_kernel(tc, x_words, x_scales, tscale, cscale, w
                 xs_window[32 * q : 32 * q + 4, :].bitcast(I32),
                 x_scales[0, 4 * q : 4 * q + 4, :].bitcast(I32),
             )
-
-        xw_window = keep.tile([P, T], I32, name="xw_window", align_bytes=64)
-        nc.sync.dma_start(xw_window[:], x_words[0].rearrange("p n t -> p (n t)").bitcast(I32))
 
         w_view = w1.rearrange("(p j) m -> p j m", j=PACK)
         w_raw = []
@@ -78,7 +79,9 @@ def tile_picked_tokscale_none_po_kernel(tc, x_words, x_scales, tscale, cscale, w
                 nc.tensor.transpose(spread[:, c, :], ts_rows[:, col : col + 1].to_broadcast([P, P]), ident[:])
             nc.scalar.copy(ts_view[:, :, 4 * b : 4 * b + 4], spread[:].rearrange("p c n -> p n c"))
 
-        xs_picked = keep.tile([P, S], U8, name="xs_picked", align_bytes=64)
+        xw_picked = keep.tile([P, S], U32, name="xw_picked", align_bytes=64)
+        nc.vector.tensor_copy(xw_picked[:], xw_window[:].bitcast(U32).indirect(offsets[:]))
+        xs_picked = keep.tile([P, S], U8, name="xs_picked", tag="words_then_bytes", align_bytes=64)
         nc.vector.tensor_copy(xs_picked[:], xs_window[:].indirect(offsets[:]))
 
         w_codes = keep.tile([P, N], U32, name="w_codes", align_bytes=64)
@@ -97,11 +100,9 @@ def tile_picked_tokscale_none_po_kernel(tc, x_words, x_scales, tscale, cscale, w
             )
 
         round_w(nc.scalar.copy, 0, 0, half_m)
-        round_w(nc.scalar.copy, 1, 0, half_m // 2)
+        round_w(nc.scalar.copy, 1, 0, SCALAR_W)
 
         n_chunks = S // CHUNK
-        xw_picked = keep.tile([P, S], U32, name="xw_picked", tag="bytes_then_words", align_bytes=64)
-        nc.vector.tensor_copy(xw_picked[:], xw_window[:].bitcast(U32).indirect(offsets[:]))
         ts_picked = []
 
         def pick_ts(c, tag):
@@ -110,7 +111,7 @@ def tile_picked_tokscale_none_po_kernel(tc, x_words, x_scales, tscale, cscale, w
             ts_picked.append(tile)
 
         pick_ts(0, "ts_picked0")
-        round_w(nc.vector.tensor_copy, 1, half_m // 2, half_m)
+        round_w(nc.vector.tensor_copy, 1, SCALAR_W, half_m)
         for h in range(2):
             for t in range(PACK):
                 cols = slice(t * P + h * half_m, t * P + (h + 1) * half_m)

@@ -21,7 +21,7 @@ PACK = 4
 W_HALF = N // 2
 CHUNK = 256
 SCALAR_LAST = 96
-SCALAR_W = 32
+SCALAR_W = 40
 
 
 def tile_picked_tokscale_none_po_kernel(tc, x_words, x_scales, tscale, cscale, w1, offs, out_0, out_1, out_2):
@@ -120,7 +120,7 @@ def tile_picked_tokscale_none_po_kernel(tc, x_words, x_scales, tscale, cscale, w
                     scales=w_scales[:, cols],
                     in_=w_bf[h][:, t * W_HALF : (t + 1) * W_HALF],
                 )
-        pick_ts(1, "w_raw0")
+        pick_ts(1, "w_raw1")
 
         y_codes = keep.tile([P, S], I32, name="y_codes", align_bytes=64)
         y_scales = keep.tile([P, S], U8, name="y_scales", align_bytes=64)

@@ -21,7 +21,7 @@ PACK = 4
 W_HALF = N // 2
 CHUNK = 256
 SCALAR_LAST = 96
-SCALAR_W = 40
+SCALAR_W = 44
 
 
 def tile_picked_tokscale_none_po_kernel(tc, x_words, x_scales, tscale, cscale, w1, offs, out_0, out_1, out_2):
@@ -36,7 +36,7 @@ def tile_picked_tokscale_none_po_kernel(tc, x_words, x_scales, tscale, cscale, w
         ts_rows = keep.tile([P, T // P], F32, name="ts_rows", tag="rows_then_w", align_bytes=64)
         nc.scalar.dma_start(ts_rows[:], tscale[0].rearrange("(n c) -> n c", c=T // P))
 
-        xw_window = keep.tile([P, T], I32, name="xw_window", tag="words_then_bytes", align_bytes=64)
+        xw_window = keep.tile([P, T], I32, name="xw_window", align_bytes=64)
         nc.sync.dma_start(xw_window[:], x_words[0].rearrange("p n t -> p (n t)").bitcast(I32))
 
         xs_window = keep.tile([P, T], U8, name="xs_window", align_bytes=64)
@@ -81,7 +81,7 @@ def tile_picked_tokscale_none_po_kernel(tc, x_words, x_scales, tscale, cscale, w
 
         xw_picked = keep.tile([P, S], U32, name="xw_picked", align_bytes=64)
         nc.vector.tensor_copy(xw_picked[:], xw_window[:].bitcast(U32).indirect(offsets[:]))
-        xs_picked = keep.tile([P, S], U8, name="xs_picked", tag="words_then_bytes", align_bytes=64)
+        xs_picked = keep.tile([P, S], U8, name="xs_picked", align_bytes=64)
         nc.vector.tensor_copy(xs_picked[:], xs_window[:].indirect(offsets[:]))
 
         w_codes = keep.tile([P, N], U32, name="w_codes", align_bytes=64)
@@ -89,7 +89,7 @@ def tile_picked_tokscale_none_po_kernel(tc, x_words, x_scales, tscale, cscale, w
         half_m = W_HALF // PACK
         w_bf = []
         for h in range(2):
-            tag = "rows_then_w" if h == 0 else "w_raw0"
+            tag = "rows_then_w" if h == 0 else "w_bf1"
             bf = keep.tile([P, W_HALF * PACK], BF16, name="w_bf%d" % h, tag=tag, align_bytes=64)
             w_bf.append(bf)
 

@@ -14,6 +14,7 @@ U8 = mybir.dt.uint8
 FP8X4 = mybir.dt.float8_e4m3fn_x4
 MULT = mybir.AluOpType.mult
 ADD = mybir.AluOpType.add
+SUBTRACT = mybir.AluOpType.subtract
 IS_EQUAL = mybir.AluOpType.is_equal
 
 P = 128
@@ -21,7 +22,8 @@ PACK = 4
 W_HALF = N // 2
 CHUNK = 256
 SCALAR_LAST = 96
-SCALAR_W = 44
+SCALAR_W = 40
+LIVE = P - 1
 
 
 def tile_picked_tokscale_none_po_kernel(tc, x_words, x_scales, tscale, cscale, w1, offs, out_0, out_1, out_2):
@@ -33,64 +35,64 @@ def tile_picked_tokscale_none_po_kernel(tc, x_words, x_scales, tscale, cscale, w
         offsets = keep.tile([P, S // 16], U16, name="offsets")
         nc.sync.dma_start(offsets[:], offs)
 
-        ts_rows = keep.tile([P, T // P], F32, name="ts_rows", tag="rows_then_w", align_bytes=64)
-        nc.scalar.dma_start(ts_rows[:], tscale[0].rearrange("(n c) -> n c", c=T // P))
-
-        xw_window = keep.tile([P, T], I32, name="xw_window", align_bytes=64)
-        nc.sync.dma_start(xw_window[:], x_words[0].rearrange("p n t -> p (n t)").bitcast(I32))
-
         xs_window = keep.tile([P, T], U8, name="xs_window", align_bytes=64)
         nc.vector.memset(xs_window[:].bitcast(I32), 0)
+
+        ts_window = keep.tile([P, T], F32, name="ts_window", align_bytes=64)
+        nc.scalar.dma_start(ts_window[LIVE : LIVE + 1, :], tscale[0:1, :])
+
+        quadrant_start = keep.tile([P, 1], F32, name="quadrant_start")
         for q in range(4):
-            engine = nc.sync if q % 2 == 0 else nc.scalar
-            engine.dma_start(
-                xs_window[32 * q : 32 * q + 4, :].bitcast(I32),
-                x_scales[0, 4 * q : 4 * q + 4, :].bitcast(I32),
-            )
+            nc.gpsimd.memset(quadrant_start[32 * q : 32 * q + 32, :], 32.0 * q)
+        ones = keep.tile([P, P], F32, name="ones")
+        nc.vector.memset(ones[:], 1.0)
+        column_count = keep.tile([P, P], F32, name="column_count", align_bytes=64)
+        nc.vector.tensor_tensor_scan(column_count[:], ones[:], ones[:], 0.0, MULT, ADD)
+        row_count = keep.tile([P, 32], F32, name="row_count", align_bytes=64)
+        nc.vector.transpose(row_count[:], column_count[:, 0:32])
+        ident = keep.tile([P, P], F32, name="ident")
+        nc.vector.tensor_scalar(ident[:], column_count[:], quadrant_start[:], row_count[:, 0:1], SUBTRACT, IS_EQUAL)
+
+        nc.gpsimd.memset(ts_window[0:LIVE, :], 0.0)
 
         w_view = w1.rearrange("(p j) m -> p j m", j=PACK)
         w_raw = []
-        for h in range(2):
+
+        def load_w(h):
             raw = keep.tile([P, PACK, W_HALF], F32, name="w_raw%d" % h, tag="w_raw%d" % h, align_bytes=64)
             nc.sync.dma_start(raw[:], w_view[:, :, h * W_HALF : (h + 1) * W_HALF])
             w_raw.append(raw)
 
+        load_w(0)
+        for q in range(4):
+            engine = nc.sync if q < 2 else nc.scalar
+            engine.dma_start(
+                xs_window[32 * q : 32 * q + 4, :].bitcast(I32),
+                x_scales[0, 4 * q : 4 * q + 4, :].bitcast(I32),
+            )
+        load_w(1)
+
+        xw_window = keep.tile([P, T], I32, name="xw_window", align_bytes=64)
+        nc.sync.dma_start(xw_window[:], x_words[0].rearrange("p n t -> p (n t)").bitcast(I32))
+
         cs = keep.tile([P, PACK], F32, name="cs")
         nc.sync.dma_start(cs[:], cscale.rearrange("(p t) o -> p (t o)", t=PACK))
 
-        ones = keep.tile([P, 32], F32, name="ones")
-        nc.vector.memset(ones[:], 1.0)
-        ident = keep.tile([P, P], F32, name="ident")
-        nc.vector.memset(ident[:], 0.0)
-        column_count = keep.tile([P, 32], F32, name="column_count", align_bytes=64)
-        nc.vector.tensor_tensor_scan(column_count[:], ones[:], ones[:], 0.0, MULT, ADD)
-        row_count = keep.tile([P, 32], F32, name="row_count", align_bytes=64)
-        nc.vector.transpose(row_count[:], column_count[:])
-        for q in range(4):
-            block = slice(32 * q, 32 * q + 32)
-            nc.vector.tensor_tensor(ident[block, block], column_count[block, :], row_count[block, :], IS_EQUAL)
-
-        ts_window = keep.tile([P, T], F32, name="ts_window", align_bytes=64)
-        ts_view = ts_window[:].rearrange("p (n c) -> p n c", c=T // P)
-        for b in range(2):
-            spread = psum.tile([P, 4, P], F32, name="spread%d" % b, tag="bank%d" % b)
-            for c in range(4):
-                col = 4 * b + c
-                nc.tensor.transpose(spread[:, c, :], ts_rows[:, col : col + 1].to_broadcast([P, P]), ident[:])
-            nc.scalar.copy(ts_view[:, :, 4 * b : 4 * b + 4], spread[:].rearrange("p c n -> p n c"))
-
-        xw_picked = keep.tile([P, S], U32, name="xw_picked", align_bytes=64)
-        nc.vector.tensor_copy(xw_picked[:], xw_window[:].bitcast(U32).indirect(offsets[:]))
+        ts_row = keep.tile([P, S], F32, name="ts_row", align_bytes=64)
+        nc.vector.tensor_copy(ts_row[:], ts_window[:].indirect(offsets[:]))
         xs_picked = keep.tile([P, S], U8, name="xs_picked", align_bytes=64)
         nc.vector.tensor_copy(xs_picked[:], xs_window[:].indirect(offsets[:]))
+
+        turned = psum.tile([P, S // P, P], F32, name="turned", tag="bank7")
+        for b in range(S // P):
+            nc.tensor.transpose(turned[:, b, :], ts_row[:, b * P : (b + 1) * P], ident[:])
 
         w_codes = keep.tile([P, N], U32, name="w_codes", align_bytes=64)
         w_scales = keep.tile([P, N], U8, name="w_scales", align_bytes=64)
         half_m = W_HALF // PACK
         w_bf = []
         for h in range(2):
-            tag = "rows_then_w" if h == 0 else "w_bf1"
-            bf = keep.tile([P, W_HALF * PACK], BF16, name="w_bf%d" % h, tag=tag, align_bytes=64)
+            bf = keep.tile([P, W_HALF * PACK], BF16, name="w_bf%d" % h, align_bytes=64)
             w_bf.append(bf)
 
         def round_w(copy, h, m0, m1):
@@ -100,18 +102,23 @@ def tile_picked_tokscale_none_po_kernel(tc, x_words, x_scales, tscale, cscale, w
             )
 
         round_w(nc.scalar.copy, 0, 0, half_m)
+
+        ts_cols = keep.tile([P, S // P], F32, name="ts_cols", tag="w_raw0", align_bytes=64)
+        nc.scalar.copy(ts_cols[:], turned[:, :, LIVE])
+        spread = psum.tile([P, S], F32, name="spread", tag="bank6")
+        for b in range(S // P):
+            nc.tensor.transpose(spread[:, b * P : (b + 1) * P], ts_cols[:, b : b + 1].to_broadcast([P, P]), ident[:])
+
         round_w(nc.scalar.copy, 1, 0, SCALAR_W)
+        round_w(nc.vector.tensor_copy, 1, SCALAR_W, half_m)
 
         n_chunks = S // CHUNK
+        ts_all = keep.tile([P, S], F32, name="ts_all", tag="w_raw1", align_bytes=64)
         ts_picked = []
+        for c in range(n_chunks):
+            nc.scalar.copy(ts_all[:, c * CHUNK : (c + 1) * CHUNK], spread[:, c * CHUNK : (c + 1) * CHUNK])
+            ts_picked.append(ts_all[:, c * CHUNK : (c + 1) * CHUNK])
 
-        def pick_ts(c, tag):
-            tile = keep.tile([P, CHUNK], F32, name="ts_picked%d" % c, tag=tag, align_bytes=64)
-            nc.vector.tensor_copy(tile[:], ts_window[:].indirect(offsets[:, c * CHUNK // 16 : (c + 1) * CHUNK // 16]))
-            ts_picked.append(tile)
-
-        pick_ts(0, "ts_picked0")
-        round_w(nc.vector.tensor_copy, 1, SCALAR_W, half_m)
         for h in range(2):
             for t in range(PACK):
                 cols = slice(t * P + h * half_m, t * P + (h + 1) * half_m)
@@ -120,7 +127,13 @@ def tile_picked_tokscale_none_po_kernel(tc, x_words, x_scales, tscale, cscale, w
                     scales=w_scales[:, cols],
                     in_=w_bf[h][:, t * W_HALF : (t + 1) * W_HALF],
                 )
-        pick_ts(1, "w_raw1")
+
+        xw_picked = keep.tile([P, S], U32, name="xw_picked", align_bytes=64)
+        for c in range(n_chunks):
+            nc.vector.tensor_copy(
+                xw_picked[:, c * CHUNK : (c + 1) * CHUNK],
+                xw_window[:].bitcast(U32).indirect(offsets[:, c * CHUNK // 16 : (c + 1) * CHUNK // 16]),
+            )
 
         y_codes = keep.tile([P, S], I32, name="y_codes", align_bytes=64)
         y_scales = keep.tile([P, S], U8, name="y_scales", align_bytes=64)
@@ -159,7 +172,7 @@ def tile_picked_tokscale_none_po_kernel(tc, x_words, x_scales, tscale, cscale, w
                     start=True,
                     stop=True,
                 )
-                nc.vector.scalar_tensor_tensor(tile[:, t, :], acc[:], cs[:, t : t + 1], ts_picked[c][:], MULT, MULT)
+                nc.vector.scalar_tensor_tensor(tile[:, t, :], acc[:], cs[:, t : t + 1], ts_picked[c], MULT, MULT)
                 if c == 0 and t < 2:
                     nc.sync.dma_start(out_rows[:, t, cols], tile[:, t, :])
                 elif t % 2 == 1:

@@ -16,6 +16,7 @@ MULT = mybir.AluOpType.mult
 ADD = mybir.AluOpType.add
 SUBTRACT = mybir.AluOpType.subtract
 IS_EQUAL = mybir.AluOpType.is_equal
+COPY = mybir.ActivationFunctionType.Copy
 
 P = 128
 PACK = 4
@@ -79,13 +80,20 @@ def tile_picked_tokscale_none_po_kernel(tc, x_words, x_scales, tscale, cscale, w
         nc.sync.dma_start(cs[:], cscale.rearrange("(p t) o -> p (t o)", t=PACK))
 
         ts_row = keep.tile([P, S], F32, name="ts_row", align_bytes=64)
-        nc.vector.tensor_copy(ts_row[:], ts_window[:].indirect(offsets[:]))
+        for h in range(2):
+            nc.vector.tensor_copy(
+                ts_row[:, h * CHUNK : (h + 1) * CHUNK],
+                ts_window[:].indirect(offsets[:, h * CHUNK // 16 : (h + 1) * CHUNK // 16]),
+            )
         xs_picked = keep.tile([P, S], U8, name="xs_picked", align_bytes=64)
         nc.vector.tensor_copy(xs_picked[:], xs_window[:].indirect(offsets[:]))
 
-        turned = psum.tile([P, S // P, P], F32, name="turned", tag="bank7")
-        for b in range(S // P):
-            nc.tensor.transpose(turned[:, b, :], ts_row[:, b * P : (b + 1) * P], ident[:])
+        turned = []
+        for h in range(2):
+            bank = psum.tile([P, 2, P], F32, name="turned%d" % h)
+            turned.append(bank)
+            for b in range(2):
+                nc.tensor.transpose(bank[:, b, :], ts_row[:, (2 * h + b) * P : (2 * h + b + 1) * P], ident[:])
 
         w_codes = keep.tile([P, N], U32, name="w_codes", align_bytes=64)
         w_scales = keep.tile([P, N], U8, name="w_scales", align_bytes=64)
@@ -103,9 +111,10 @@ def tile_picked_tokscale_none_po_kernel(tc, x_words, x_scales, tscale, cscale, w
 
         round_w(nc.scalar.copy, 0, 0, half_m)
 
-        ts_cols = keep.tile([P, S // P], F32, name="ts_cols", tag="w_raw0", align_bytes=64)
-        nc.scalar.copy(ts_cols[:], turned[:, :, LIVE])
-        spread = psum.tile([P, S], F32, name="spread", tag="bank6")
+        ts_cols = keep.tile([P, S // P], F32, name="ts_cols", align_bytes=64)
+        for h in range(2):
+            nc.scalar.copy(ts_cols[:, 2 * h : 2 * h + 2], turned[h][:, :, LIVE])
+        spread = psum.tile([P, S], F32, name="spread")
         for b in range(S // P):
             nc.tensor.transpose(spread[:, b * P : (b + 1) * P], ts_cols[:, b : b + 1].to_broadcast([P, P]), ident[:])
 
@@ -113,11 +122,12 @@ def tile_picked_tokscale_none_po_kernel(tc, x_words, x_scales, tscale, cscale, w
         round_w(nc.vector.tensor_copy, 1, SCALAR_W, half_m)
 
         n_chunks = S // CHUNK
-        ts_all = keep.tile([P, S], F32, name="ts_all", tag="w_raw1", align_bytes=64)
-        ts_picked = []
+        factor = []
         for c in range(n_chunks):
-            nc.scalar.copy(ts_all[:, c * CHUNK : (c + 1) * CHUNK], spread[:, c * CHUNK : (c + 1) * CHUNK])
-            ts_picked.append(ts_all[:, c * CHUNK : (c + 1) * CHUNK])
+            tile = keep.tile([P, PACK, CHUNK], F32, name="factor%d" % c, align_bytes=64)
+            factor.append(tile)
+            for t in range(PACK):
+                nc.scalar.activation(tile[:, t, :], spread[:, c * CHUNK : (c + 1) * CHUNK], COPY, scale=cs[:, t : t + 1])
 
         for h in range(2):
             for t in range(PACK):
@@ -161,22 +171,20 @@ def tile_picked_tokscale_none_po_kernel(tc, x_words, x_scales, tscale, cscale, w
             cols = slice(c * CHUNK, (c + 1) * CHUNK)
             tile = keep.tile([P, PACK, CHUNK], F32, name="y%d" % c, align_bytes=64)
             y.append(tile)
-            for t in range(PACK):
-                acc = psum.tile([P, CHUNK], F32, name="acc%d_%d" % (c, t), tag="bank%d" % (c * PACK + t))
-                nc.tensor.matmul_mx(
-                    out=acc[:],
-                    lhsT=w_codes[:, t * P : (t + 1) * P].bitcast(FP8X4),
-                    lhsT_scale=w_scales[:, t * P : (t + 1) * P],
-                    rhs=xw_picked[:, cols].bitcast(FP8X4),
-                    rhs_scale=xs_picked[:, cols],
-                    start=True,
-                    stop=True,
-                )
-                nc.vector.scalar_tensor_tensor(tile[:, t, :], acc[:], cs[:, t : t + 1], ts_picked[c], MULT, MULT)
-                if c == 0 and t < 2:
-                    nc.sync.dma_start(out_rows[:, t, cols], tile[:, t, :])
-                elif t % 2 == 1:
-                    nc.sync.dma_start(out_rows[:, t - 1 : t + 1, cols], tile[:, t - 1 : t + 1, :])
+            for t0, t1 in ([(0, 1), (1, 2), (2, 4)] if c == 0 else [(0, 2), (2, 4)]):
+                acc = psum.tile([P, t1 - t0, CHUNK], F32, name="acc%d_%d" % (c, t0))
+                for t in range(t0, t1):
+                    nc.tensor.matmul_mx(
+                        out=acc[:, t - t0, :],
+                        lhsT=w_codes[:, t * P : (t + 1) * P].bitcast(FP8X4),
+                        lhsT_scale=w_scales[:, t * P : (t + 1) * P],
+                        rhs=xw_picked[:, cols].bitcast(FP8X4),
+                        rhs_scale=xs_picked[:, cols],
+                        start=True,
+                        stop=True,
+                    )
+                nc.vector.tensor_tensor(tile[:, t0:t1, :], acc[:], factor[c][:, t0:t1, :], MULT)
+                nc.sync.dma_start(out_rows[:, t0:t1, cols], tile[:, t0:t1, :])
             round_y(nc.scalar.copy, c, 0, CHUNK if c == 0 else SCALAR_LAST)
 
         round_y(nc.vector.tensor_copy, 1, SCALAR_LAST, CHUNK)

@@ -22,7 +22,7 @@ P = 128
 PACK = 4
 W_HALF = N // 2
 CHUNK = 256
-SCALAR_LAST = 96
+SCALAR_LAST = 112
 SCALAR_W = 40
 LIVE = P - 1
 
@@ -139,10 +139,10 @@ def tile_picked_tokscale_none_po_kernel(tc, x_words, x_scales, tscale, cscale, w
                 )
 
         xw_picked = keep.tile([P, S], U32, name="xw_picked", align_bytes=64)
-        for c in range(n_chunks):
+        for s0, s1 in ((0, P), (P, CHUNK), (CHUNK, S)):
             nc.vector.tensor_copy(
-                xw_picked[:, c * CHUNK : (c + 1) * CHUNK],
-                xw_window[:].bitcast(U32).indirect(offsets[:, c * CHUNK // 16 : (c + 1) * CHUNK // 16]),
+                xw_picked[:, s0:s1],
+                xw_window[:].bitcast(U32).indirect(offsets[:, s0 // 16 : s1 // 16]),
             )
 
         y_codes = keep.tile([P, S], I32, name="y_codes", align_bytes=64)
@@ -158,38 +158,42 @@ def tile_picked_tokscale_none_po_kernel(tc, x_words, x_scales, tscale, cscale, w
                 y[c][:, :, s0:s1].rearrange("p t (g i) -> p g t i", i=4),
             )
 
-        def quantize_y(c):
-            cols = slice(c * CHUNK, (c + 1) * CHUNK)
+        def quantize_y(s0, s1):
             nc.vector.quantize_mx(
-                out=y_codes[:, cols].bitcast(FP8X4),
-                scales=y_scales[:, cols],
-                in_=y_bf[:, c * CHUNK * PACK : (c + 1) * CHUNK * PACK],
+                out=y_codes[:, s0:s1].bitcast(FP8X4),
+                scales=y_scales[:, s0:s1],
+                in_=y_bf[:, s0 * PACK : s1 * PACK],
             )
-            nc.sync.dma_start(out_words[:, cols], y_codes[:, cols])
 
         for c in range(n_chunks):
-            cols = slice(c * CHUNK, (c + 1) * CHUNK)
             tile = keep.tile([P, PACK, CHUNK], F32, name="y%d" % c, align_bytes=64)
             y.append(tile)
-            for t0, t1 in ([(0, 1), (1, 2), (2, 4)] if c == 0 else [(0, 2), (2, 4)]):
-                acc = psum.tile([P, t1 - t0, CHUNK], F32, name="acc%d_%d" % (c, t0))
+            banks = [(0, 2, 0, P), (2, PACK, 0, P), (0, PACK, P, CHUNK)] if c == 0 else [(0, 2, 0, CHUNK), (2, PACK, 0, CHUNK)]
+            for b, (t0, t1, s0, s1) in enumerate(banks):
+                tokens = slice(c * CHUNK + s0, c * CHUNK + s1)
+                acc = psum.tile([P, t1 - t0, s1 - s0], F32, name="acc%d_%d" % (c, b))
                 for t in range(t0, t1):
                     nc.tensor.matmul_mx(
                         out=acc[:, t - t0, :],
                         lhsT=w_codes[:, t * P : (t + 1) * P].bitcast(FP8X4),
                         lhsT_scale=w_scales[:, t * P : (t + 1) * P],
-                        rhs=xw_picked[:, cols].bitcast(FP8X4),
-                        rhs_scale=xs_picked[:, cols],
+                        rhs=xw_picked[:, tokens].bitcast(FP8X4),
+                        rhs_scale=xs_picked[:, tokens],
                         start=True,
                         stop=True,
                     )
-                nc.vector.tensor_tensor(tile[:, t0:t1, :], acc[:], factor[c][:, t0:t1, :], MULT)
-                nc.sync.dma_start(out_rows[:, t0:t1, cols], tile[:, t0:t1, :])
-            round_y(nc.scalar.copy, c, 0, CHUNK if c == 0 else SCALAR_LAST)
+                nc.vector.tensor_tensor(tile[:, t0:t1, s0:s1], acc[:], factor[c][:, t0:t1, s0:s1], MULT)
+                nc.sync.dma_start(out_rows[:, t0:t1, tokens], tile[:, t0:t1, s0:s1])
+                if c == 0 and t1 == PACK:
+                    round_y(nc.scalar.copy, c, s0, s1)
+        round_y(nc.scalar.copy, 1, 0, SCALAR_LAST)
 
+        quantize_y(0, P)
         round_y(nc.vector.tensor_copy, 1, SCALAR_LAST, CHUNK)
-        quantize_y(0)
-        quantize_y(1)
+        quantize_y(P, CHUNK)
+        nc.sync.dma_start(out_words[:, :CHUNK], y_codes[:, :CHUNK])
+        quantize_y(CHUNK, S)
+        nc.sync.dma_start(out_words[:, CHUNK:], y_codes[:, CHUNK:])
 
         for q in range(4):
             engine = nc.sync if q == 0 else nc.scalar

@@ -42,19 +42,19 @@ def tile_picked_tokscale_none_po_kernel(tc, x_words, x_scales, tscale, cscale, w
         ts_window = keep.tile([P, T], F32, name="ts_window", align_bytes=64)
         nc.scalar.dma_start(ts_window[LIVE : LIVE + 1, :], tscale[0:1, :])
 
+        ones = keep.tile([P, P], F32, name="ones")
+        nc.gpsimd.memset(ones[:], 1.0)
         quadrant_start = keep.tile([P, 1], F32, name="quadrant_start")
         for q in range(4):
             nc.gpsimd.memset(quadrant_start[32 * q : 32 * q + 32, :], 32.0 * q)
-        ones = keep.tile([P, P], F32, name="ones")
-        nc.vector.memset(ones[:], 1.0)
         column_count = keep.tile([P, P], F32, name="column_count", align_bytes=64)
         nc.vector.tensor_tensor_scan(column_count[:], ones[:], ones[:], 0.0, MULT, ADD)
+        nc.vector.memset(ts_window[0:LIVE, : T // 2], 0.0)
         row_count = keep.tile([P, 32], F32, name="row_count", align_bytes=64)
         nc.vector.transpose(row_count[:], column_count[:, 0:32])
+        nc.vector.memset(ts_window[0:LIVE, T // 2 :], 0.0)
         ident = keep.tile([P, P], F32, name="ident")
         nc.vector.tensor_scalar(ident[:], column_count[:], quadrant_start[:], row_count[:, 0:1], SUBTRACT, IS_EQUAL)
-
-        nc.gpsimd.memset(ts_window[0:LIVE, :], 0.0)
 
         w_view = w1.rearrange("(p j) m -> p j m", j=PACK)
         w_raw = []

@@ -23,7 +23,7 @@ PACK = 4
 W_HALF = N // 2
 CHUNK = 256
 SCALAR_LAST = 112
-SCALAR_W = 40
+SCALAR_W = 34
 LIVE = P - 1
 
 
@@ -66,7 +66,7 @@ def tile_picked_tokscale_none_po_kernel(tc, x_words, x_scales, tscale, cscale, w
 
         load_w(0)
         for q in range(4):
-            engine = nc.sync if q < 2 else nc.scalar
+            engine = nc.sync if q % 2 == 0 else nc.scalar
             engine.dma_start(
                 xs_window[32 * q : 32 * q + 4, :].bitcast(I32),
                 x_scales[0, 4 * q : 4 * q + 4, :].bitcast(I32),
@@ -88,12 +88,9 @@ def tile_picked_tokscale_none_po_kernel(tc, x_words, x_scales, tscale, cscale, w
         xs_picked = keep.tile([P, S], U8, name="xs_picked", align_bytes=64)
         nc.vector.tensor_copy(xs_picked[:], xs_window[:].indirect(offsets[:]))
 
-        turned = []
-        for h in range(2):
-            bank = psum.tile([P, 2, P], F32, name="turned%d" % h)
-            turned.append(bank)
-            for b in range(2):
-                nc.tensor.transpose(bank[:, b, :], ts_row[:, (2 * h + b) * P : (2 * h + b + 1) * P], ident[:])
+        turned = psum.tile([P, S // P, P], F32, name="turned")
+        for b in range(S // P):
+            nc.tensor.transpose(turned[:, b, :], ts_row[:, b * P : (b + 1) * P], ident[:])
 
         w_codes = keep.tile([P, N], U32, name="w_codes", align_bytes=64)
         w_scales = keep.tile([P, N], U8, name="w_scales", align_bytes=64)
@@ -112,8 +109,7 @@ def tile_picked_tokscale_none_po_kernel(tc, x_words, x_scales, tscale, cscale, w
         round_w(nc.scalar.copy, 0, 0, half_m)
 
         ts_cols = keep.tile([P, S // P], F32, name="ts_cols", align_bytes=64)
-        for h in range(2):
-            nc.scalar.copy(ts_cols[:, 2 * h : 2 * h + 2], turned[h][:, :, LIVE])
+        nc.scalar.copy(ts_cols[:], turned[:, :, LIVE])
         spread = psum.tile([P, S], F32, name="spread")
         for b in range(S // P):
             nc.tensor.transpose(spread[:, b * P : (b + 1) * P], ts_cols[:, b : b + 1].to_broadcast([P, P]), ident[:])

@@ -22,8 +22,8 @@ P = 128
 PACK = 4
 W_HALF = N // 2
 CHUNK = 256
-SCALAR_LAST = 112
-SCALAR_W = 34
+SCALAR_LAST = 128
+SCALAR_W = 40
 LIVE = P - 1
 
 
@@ -66,7 +66,7 @@ def tile_picked_tokscale_none_po_kernel(tc, x_words, x_scales, tscale, cscale, w
 
         load_w(0)
         for q in range(4):
-            engine = nc.sync if q % 2 == 0 else nc.scalar
+            engine = nc.sync if q < 2 else nc.scalar
             engine.dma_start(
                 xs_window[32 * q : 32 * q + 4, :].bitcast(I32),
                 x_scales[0, 4 * q : 4 * q + 4, :].bitcast(I32),
@@ -134,6 +134,18 @@ def tile_picked_tokscale_none_po_kernel(tc, x_words, x_scales, tscale, cscale, w
                     in_=w_bf[h][:, t * W_HALF : (t + 1) * W_HALF],
                 )
 
+        unused = psum.tile([P, 2, CHUNK], F32, name="unused")
+        for i in range(2):
+            nc.tensor.matmul_mx(
+                out=unused[:, i, :],
+                lhsT=w_codes[:, :P].bitcast(FP8X4),
+                lhsT_scale=w_scales[:, :P],
+                rhs=w_codes[:, :CHUNK].bitcast(FP8X4),
+                rhs_scale=w_scales[:, :CHUNK],
+                start=True,
+                stop=True,
+            )
+
         xw_picked = keep.tile([P, S], U32, name="xw_picked", align_bytes=64)
         for s0, s1 in ((0, P), (P, CHUNK), (CHUNK, S)):
             nc.vector.tensor_copy(
@@ -184,11 +196,11 @@ def tile_picked_tokscale_none_po_kernel(tc, x_words, x_scales, tscale, cscale, w
                     round_y(nc.scalar.copy, c, s0, s1)
         round_y(nc.scalar.copy, 1, 0, SCALAR_LAST)
 
-        quantize_y(0, P)
-        round_y(nc.vector.tensor_copy, 1, SCALAR_LAST, CHUNK)
-        quantize_y(P, CHUNK)
+        quantize_y(0, CHUNK)
         nc.sync.dma_start(out_words[:, :CHUNK], y_codes[:, :CHUNK])
-        quantize_y(CHUNK, S)
+        round_y(nc.vector.tensor_copy, 1, SCALAR_LAST, CHUNK)
+        quantize_y(CHUNK, CHUNK + SCALAR_LAST)
+        quantize_y(CHUNK + SCALAR_LAST, S)
         nc.sync.dma_start(out_words[:, CHUNK:], y_codes[:, CHUNK:])
 
         for q in range(4):

@@ -73,11 +73,11 @@ def tile_picked_tokscale_none_po_kernel(tc, x_words, x_scales, tscale, cscale, w
             )
         load_w(1)
 
-        xw_window = keep.tile([P, T], I32, name="xw_window", align_bytes=64)
-        nc.sync.dma_start(xw_window[:], x_words[0].rearrange("p n t -> p (n t)").bitcast(I32))
-
         cs = keep.tile([P, PACK], F32, name="cs")
         nc.sync.dma_start(cs[:], cscale.rearrange("(p t) o -> p (t o)", t=PACK))
+
+        xw_window = keep.tile([P, T], I32, name="xw_window", align_bytes=64)
+        nc.sync.dma_start(xw_window[:], x_words[0].rearrange("p n t -> p (n t)").bitcast(I32))
 
         ts_row = keep.tile([P, S], F32, name="ts_row", align_bytes=64)
         for h in range(2):
@@ -133,18 +133,6 @@ def tile_picked_tokscale_none_po_kernel(tc, x_words, x_scales, tscale, cscale, w
                     scales=w_scales[:, cols],
                     in_=w_bf[h][:, t * W_HALF : (t + 1) * W_HALF],
                 )
-
-        unused = psum.tile([P, 2, CHUNK], F32, name="unused")
-        for i in range(2):
-            nc.tensor.matmul_mx(
-                out=unused[:, i, :],
-                lhsT=w_codes[:, :P].bitcast(FP8X4),
-                lhsT_scale=w_scales[:, :P],
-                rhs=w_codes[:, :CHUNK].bitcast(FP8X4),
-                rhs_scale=w_scales[:, :CHUNK],
-                start=True,
-                stop=True,
-            )
 
         xw_picked = keep.tile([P, S], U32, name="xw_picked", align_bytes=64)
         for s0, s1 in ((0, P), (P, CHUNK), (CHUNK, S)):

@@ -23,7 +23,7 @@ PACK = 4
 W_HALF = N // 2
 CHUNK = 256
 SCALAR_LAST = 128
-SCALAR_W = 40
+SCALAR_W = (40, 46)
 LIVE = P - 1
 
 
@@ -59,19 +59,19 @@ def tile_picked_tokscale_none_po_kernel(tc, x_words, x_scales, tscale, cscale, w
         w_view = w1.rearrange("(p j) m -> p j m", j=PACK)
         w_raw = []
 
-        def load_w(h):
+        def load_w(engine, h):
             raw = keep.tile([P, PACK, W_HALF], F32, name="w_raw%d" % h, tag="w_raw%d" % h, align_bytes=64)
-            nc.sync.dma_start(raw[:], w_view[:, :, h * W_HALF : (h + 1) * W_HALF])
+            engine.dma_start(raw[:], w_view[:, :, h * W_HALF : (h + 1) * W_HALF])
             w_raw.append(raw)
 
-        load_w(0)
+        load_w(nc.sync, 0)
         for q in range(4):
             engine = nc.sync if q < 2 else nc.scalar
             engine.dma_start(
                 xs_window[32 * q : 32 * q + 4, :].bitcast(I32),
                 x_scales[0, 4 * q : 4 * q + 4, :].bitcast(I32),
             )
-        load_w(1)
+        load_w(nc.scalar, 1)
 
         cs = keep.tile([P, PACK], F32, name="cs")
         nc.sync.dma_start(cs[:], cscale.rearrange("(p t) o -> p (t o)", t=PACK))
@@ -85,8 +85,6 @@ def tile_picked_tokscale_none_po_kernel(tc, x_words, x_scales, tscale, cscale, w
                 ts_row[:, h * CHUNK : (h + 1) * CHUNK],
                 ts_window[:].indirect(offsets[:, h * CHUNK // 16 : (h + 1) * CHUNK // 16]),
             )
-        xs_picked = keep.tile([P, S], U8, name="xs_picked", align_bytes=64)
-        nc.vector.tensor_copy(xs_picked[:], xs_window[:].indirect(offsets[:]))
 
         turned = psum.tile([P, S // P, P], F32, name="turned")
         for b in range(S // P):
@@ -106,7 +104,10 @@ def tile_picked_tokscale_none_po_kernel(tc, x_words, x_scales, tscale, cscale, w
                 w_raw[h][:].rearrange("p j (m t) -> p m j t", t=PACK)[:, m0:m1],
             )
 
-        round_w(nc.scalar.copy, 0, 0, half_m)
+        round_w(nc.scalar.copy, 0, 0, SCALAR_W[0])
+        round_w(nc.vector.tensor_copy, 0, SCALAR_W[0], half_m)
+        xs_picked = keep.tile([P, S], U8, name="xs_picked", align_bytes=64)
+        nc.vector.tensor_copy(xs_picked[:], xs_window[:].indirect(offsets[:]))
 
         ts_cols = keep.tile([P, S // P], F32, name="ts_cols", align_bytes=64)
         nc.scalar.copy(ts_cols[:], turned[:, :, LIVE])
@@ -114,8 +115,8 @@ def tile_picked_tokscale_none_po_kernel(tc, x_words, x_scales, tscale, cscale, w
         for b in range(S // P):
             nc.tensor.transpose(spread[:, b * P : (b + 1) * P], ts_cols[:, b : b + 1].to_broadcast([P, P]), ident[:])
 
-        round_w(nc.scalar.copy, 1, 0, SCALAR_W)
-        round_w(nc.vector.tensor_copy, 1, SCALAR_W, half_m)
+        round_w(nc.scalar.copy, 1, 0, SCALAR_W[1])
+        round_w(nc.vector.tensor_copy, 1, SCALAR_W[1], half_m)
 
         n_chunks = S // CHUNK
         factor = []
@@ -125,21 +126,30 @@ def tile_picked_tokscale_none_po_kernel(tc, x_words, x_scales, tscale, cscale, w
             for t in range(PACK):
                 nc.scalar.activation(tile[:, t, :], spread[:, c * CHUNK : (c + 1) * CHUNK], COPY, scale=cs[:, t : t + 1])
 
-        for h in range(2):
-            for t in range(PACK):
-                cols = slice(t * P + h * half_m, t * P + (h + 1) * half_m)
-                nc.vector.quantize_mx(
-                    out=w_codes[:, cols].bitcast(FP8X4),
-                    scales=w_scales[:, cols],
-                    in_=w_bf[h][:, t * W_HALF : (t + 1) * W_HALF],
-                )
+        def quantize_w(h, t):
+            cols = slice(t * P + h * half_m, t * P + (h + 1) * half_m)
+            nc.vector.quantize_mx(
+                out=w_codes[:, cols].bitcast(FP8X4),
+                scales=w_scales[:, cols],
+                in_=w_bf[h][:, t * W_HALF : (t + 1) * W_HALF],
+            )
 
-        xw_picked = keep.tile([P, S], U32, name="xw_picked", align_bytes=64)
-        for s0, s1 in ((0, P), (P, CHUNK), (CHUNK, S)):
+        xw_picked = keep.tile([P, S], U32, name="xw_picked", tag="w_raw1", align_bytes=64)
+
+        def gather_words(s0, s1):
             nc.vector.tensor_copy(
                 xw_picked[:, s0:s1],
                 xw_window[:].bitcast(U32).indirect(offsets[:, s0 // 16 : s1 // 16]),
             )
+
+        for t in range(PACK):
+            quantize_w(0, t)
+        quantize_w(1, 0)
+        gather_words(0, P)
+        for t in range(1, PACK):
+            quantize_w(1, t)
+        gather_words(P, CHUNK)
+        gather_words(CHUNK, S)
 
         y_codes = keep.tile([P, S], I32, name="y_codes", align_bytes=64)
         y_scales = keep.tile([P, S], U8, name="y_scales", align_bytes=64)

@@ -22,8 +22,8 @@ P = 128
 PACK = 4
 W_HALF = N // 2
 CHUNK = 256
-SCALAR_LAST = 128
-SCALAR_W = (40, 46)
+SCALAR_LAST = 64
+SCALAR_W = (40, 40)
 LIVE = P - 1
 
 
@@ -174,7 +174,7 @@ def tile_picked_tokscale_none_po_kernel(tc, x_words, x_scales, tscale, cscale, w
         for c in range(n_chunks):
             tile = keep.tile([P, PACK, CHUNK], F32, name="y%d" % c, align_bytes=64)
             y.append(tile)
-            banks = [(0, 2, 0, P), (2, PACK, 0, P), (0, PACK, P, CHUNK)] if c == 0 else [(0, 2, 0, CHUNK), (2, PACK, 0, CHUNK)]
+            banks = [(0, 2, 0, P), (2, PACK, 0, P), (0, PACK, P, CHUNK)] if c == 0 else [(0, PACK, 0, P), (0, PACK, P, CHUNK)]
             for b, (t0, t1, s0, s1) in enumerate(banks):
                 tokens = slice(c * CHUNK + s0, c * CHUNK + s1)
                 acc = psum.tile([P, t1 - t0, s1 - s0], F32, name="acc%d_%d" % (c, b))
@@ -190,15 +190,14 @@ def tile_picked_tokscale_none_po_kernel(tc, x_words, x_scales, tscale, cscale, w
                     )
                 nc.vector.tensor_tensor(tile[:, t0:t1, s0:s1], acc[:], factor[c][:, t0:t1, s0:s1], MULT)
                 nc.sync.dma_start(out_rows[:, t0:t1, tokens], tile[:, t0:t1, s0:s1])
-                if c == 0 and t1 == PACK:
-                    round_y(nc.scalar.copy, c, s0, s1)
-        round_y(nc.scalar.copy, 1, 0, SCALAR_LAST)
+                if t1 == PACK:
+                    round_y(nc.scalar.copy, c, s0, s1 if (c, s0) != (1, P) else P + SCALAR_LAST)
 
         quantize_y(0, CHUNK)
         nc.sync.dma_start(out_words[:, :CHUNK], y_codes[:, :CHUNK])
-        round_y(nc.vector.tensor_copy, 1, SCALAR_LAST, CHUNK)
-        quantize_y(CHUNK, CHUNK + SCALAR_LAST)
-        quantize_y(CHUNK + SCALAR_LAST, S)
+        round_y(nc.vector.tensor_copy, 1, P + SCALAR_LAST, CHUNK)
+        quantize_y(CHUNK, CHUNK + P)
+        quantize_y(CHUNK + P, S)
         nc.sync.dma_start(out_words[:, CHUNK:], y_codes[:, CHUNK:])
 
         for q in range(4):

@@ -15,7 +15,7 @@ FP8X4 = mybir.dt.float8_e4m3fn_x4
 MULT = mybir.AluOpType.mult
 ADD = mybir.AluOpType.add
 SUBTRACT = mybir.AluOpType.subtract
-IS_EQUAL = mybir.AluOpType.is_equal
+NOT_EQUAL = mybir.AluOpType.not_equal
 COPY = mybir.ActivationFunctionType.Copy
 
 P = 128
@@ -23,7 +23,8 @@ PACK = 4
 W_HALF = N // 2
 CHUNK = 256
 SCALAR_LAST = 64
-SCALAR_W = (40, 40)
+SCALAR_LATE = 48
+SCALE_ROW0 = P - 16
 LIVE = P - 1
 
 
@@ -36,42 +37,18 @@ def tile_picked_tokscale_none_po_kernel(tc, x_words, x_scales, tscale, cscale, w
         offsets = keep.tile([P, S // 16], U16, name="offsets")
         nc.sync.dma_start(offsets[:], offs)
 
-        xs_window = keep.tile([P, T], U8, name="xs_window", align_bytes=64)
-        nc.vector.memset(xs_window[:].bitcast(I32), 0)
-
         ts_window = keep.tile([P, T], F32, name="ts_window", align_bytes=64)
         nc.scalar.dma_start(ts_window[LIVE : LIVE + 1, :], tscale[0:1, :])
 
-        ones = keep.tile([P, P], F32, name="ones")
-        nc.gpsimd.memset(ones[:], 1.0)
-        quadrant_start = keep.tile([P, 1], F32, name="quadrant_start")
-        for q in range(4):
-            nc.gpsimd.memset(quadrant_start[32 * q : 32 * q + 32, :], 32.0 * q)
-        column_count = keep.tile([P, P], F32, name="column_count", align_bytes=64)
-        nc.vector.tensor_tensor_scan(column_count[:], ones[:], ones[:], 0.0, MULT, ADD)
-        nc.vector.memset(ts_window[0:LIVE, : T // 2], 0.0)
-        row_count = keep.tile([P, 32], F32, name="row_count", align_bytes=64)
-        nc.vector.transpose(row_count[:], column_count[:, 0:32])
-        nc.vector.memset(ts_window[0:LIVE, T // 2 :], 0.0)
-        ident = keep.tile([P, P], F32, name="ident")
-        nc.vector.tensor_scalar(ident[:], column_count[:], quadrant_start[:], row_count[:, 0:1], SUBTRACT, IS_EQUAL)
+        xs_window = keep.tile([P, T], U8, name="xs_window", align_bytes=64)
+        nc.sync.dma_start(xs_window[SCALE_ROW0:, :].bitcast(I32), x_scales[0].bitcast(I32))
 
         w_view = w1.rearrange("(p j) m -> p j m", j=PACK)
         w_raw = []
-
-        def load_w(engine, h):
-            raw = keep.tile([P, PACK, W_HALF], F32, name="w_raw%d" % h, tag="w_raw%d" % h, align_bytes=64)
-            engine.dma_start(raw[:], w_view[:, :, h * W_HALF : (h + 1) * W_HALF])
+        for u in range(2):
+            raw = keep.tile([P, 2, N], F32, name="w_raw%d" % u, align_bytes=64)
+            nc.sync.dma_start(raw[:], w_view[:, 2 * u : 2 * u + 2, :])
             w_raw.append(raw)
-
-        load_w(nc.sync, 0)
-        for q in range(4):
-            engine = nc.sync if q < 2 else nc.scalar
-            engine.dma_start(
-                xs_window[32 * q : 32 * q + 4, :].bitcast(I32),
-                x_scales[0, 4 * q : 4 * q + 4, :].bitcast(I32),
-            )
-        load_w(nc.scalar, 1)
 
         cs = keep.tile([P, PACK], F32, name="cs")
         nc.sync.dma_start(cs[:], cscale.rearrange("(p t) o -> p (t o)", t=PACK))
@@ -79,16 +56,52 @@ def tile_picked_tokscale_none_po_kernel(tc, x_words, x_scales, tscale, cscale, w
         xw_window = keep.tile([P, T], I32, name="xw_window", align_bytes=64)
         nc.sync.dma_start(xw_window[:], x_words[0].rearrange("p n t -> p (n t)").bitcast(I32))
 
-        ts_row = keep.tile([P, S], F32, name="ts_row", align_bytes=64)
-        for h in range(2):
-            nc.vector.tensor_copy(
-                ts_row[:, h * CHUNK : (h + 1) * CHUNK],
-                ts_window[:].indirect(offsets[:, h * CHUNK // 16 : (h + 1) * CHUNK // 16]),
+        ones = keep.tile([P, P], F32, name="ones")
+        nc.gpsimd.memset(ones[:], 1.0)
+        quadrant_start = keep.tile([P, 1], F32, name="quadrant_start")
+        for q in range(4):
+            nc.gpsimd.memset(quadrant_start[32 * q : 32 * q + 32, :], 32.0 * q)
+        nc.vector.memset(xs_window[0:SCALE_ROW0, :].bitcast(I32), 0)
+        column_count = keep.tile([P, P], F32, name="column_count", align_bytes=64)
+        nc.vector.tensor_tensor_scan(column_count[:], ones[:], ones[:], 0.0, MULT, ADD)
+        nc.vector.memset(ts_window[0:LIVE, : T // 2], 0.0)
+        row_count = keep.tile([P, 32], F32, name="row_count", align_bytes=64)
+        nc.vector.transpose(row_count[:], column_count[:, 0:32])
+        nc.vector.memset(ts_window[0:LIVE, T // 2 :], 0.0)
+        ident = keep.tile([P, P], F32, name="ident")
+        off_diagonal = keep.tile([P, P], F32, name="off_diagonal")
+        nc.vector.tensor_scalar(off_diagonal[:], column_count[:], quadrant_start[:], row_count[:, 0:1], SUBTRACT, NOT_EQUAL)
+        nc.scalar.activation(ident[:], off_diagonal[:], COPY, scale=-1.0, bias=1.0)
+        xs_placed = keep.tile([P, S], U8, name="xs_placed", align_bytes=64)
+        nc.vector.memset(xs_placed[:].bitcast(I32), 0)
+
+        xs_picked = keep.tile([P, S], U8, name="xs_picked", align_bytes=64)
+        nc.vector.tensor_copy(xs_picked[:], xs_window[:].indirect(offsets[:]))
+        for q in range(4):
+            nc.sync.dma_start(
+                xs_placed[32 * q : 32 * q + 4, :].bitcast(I32),
+                xs_picked[SCALE_ROW0 + 4 * q : SCALE_ROW0 + 4 * q + 4, :].bitcast(I32),
             )
 
-        turned = psum.tile([P, S // P, P], F32, name="turned")
-        for b in range(S // P):
-            nc.tensor.transpose(turned[:, b, :], ts_row[:, b * P : (b + 1) * P], ident[:])
+        ts_row = keep.tile([P, S], F32, name="ts_row", align_bytes=64)
+        for h in range(2):
+            nc.scalar.activation(
+                ts_row[:, h * CHUNK : (h + 1) * CHUNK],
+                ts_window[:].indirect(offsets[:, h * CHUNK // 16 : (h + 1) * CHUNK // 16]),
+                COPY,
+            )
+
+        spread = []
+        for h in range(2):
+            turned = psum.tile([P, 2, P], F32, name="turned%d" % h, tag="turned%d" % h)
+            for b in range(2):
+                nc.tensor.transpose(turned[:, b, :], ts_row[:, (2 * h + b) * P : (2 * h + b + 1) * P], ident[:])
+            ts_cols = keep.tile([P, 2], F32, name="ts_cols%d" % h, align_bytes=64)
+            nc.scalar.copy(ts_cols[:], turned[:, :, LIVE])
+            bank = psum.tile([P, CHUNK], F32, name="spread%d" % h)
+            spread.append(bank)
+            for b in range(2):
+                nc.tensor.transpose(bank[:, b * P : (b + 1) * P], ts_cols[:, b : b + 1].to_broadcast([P, P]), ident[:])
 
         w_codes = keep.tile([P, N], U32, name="w_codes", align_bytes=64)
         w_scales = keep.tile([P, N], U8, name="w_scales", align_bytes=64)
@@ -98,25 +111,17 @@ def tile_picked_tokscale_none_po_kernel(tc, x_words, x_scales, tscale, cscale, w
             bf = keep.tile([P, W_HALF * PACK], BF16, name="w_bf%d" % h, align_bytes=64)
             w_bf.append(bf)
 
-        def round_w(copy, h, m0, m1):
+        def round_w(copy, u, h, m0, m1):
             copy(
-                w_bf[h][:].rearrange("p (t m j) -> p m j t", t=PACK, j=PACK)[:, m0:m1],
-                w_raw[h][:].rearrange("p j (m t) -> p m j t", t=PACK)[:, m0:m1],
+                w_bf[h][:].rearrange("p (t m u j) -> p u m j t", t=PACK, u=2, j=2)[:, u, m0:m1],
+                w_raw[u][:, :, h * W_HALF : (h + 1) * W_HALF].rearrange("p j (m t) -> p m j t", t=PACK)[:, m0:m1],
             )
 
-        round_w(nc.scalar.copy, 0, 0, SCALAR_W[0])
-        round_w(nc.vector.tensor_copy, 0, SCALAR_W[0], half_m)
-        xs_picked = keep.tile([P, S], U8, name="xs_picked", align_bytes=64)
-        nc.vector.tensor_copy(xs_picked[:], xs_window[:].indirect(offsets[:]))
-
-        ts_cols = keep.tile([P, S // P], F32, name="ts_cols", align_bytes=64)
-        nc.scalar.copy(ts_cols[:], turned[:, :, LIVE])
-        spread = psum.tile([P, S], F32, name="spread")
-        for b in range(S // P):
-            nc.tensor.transpose(spread[:, b * P : (b + 1) * P], ts_cols[:, b : b + 1].to_broadcast([P, P]), ident[:])
-
-        round_w(nc.scalar.copy, 1, 0, SCALAR_W[1])
-        round_w(nc.vector.tensor_copy, 1, SCALAR_W[1], half_m)
+        for h in range(2):
+            round_w(nc.vector.tensor_copy, 0, h, 0, half_m)
+        round_w(nc.vector.tensor_copy, 1, 0, 0, half_m)
+        round_w(nc.scalar.copy, 1, 1, 0, SCALAR_LATE)
+        round_w(nc.vector.tensor_copy, 1, 1, SCALAR_LATE, half_m)
 
         n_chunks = S // CHUNK
         factor = []
@@ -124,7 +129,7 @@ def tile_picked_tokscale_none_po_kernel(tc, x_words, x_scales, tscale, cscale, w
             tile = keep.tile([P, PACK, CHUNK], F32, name="factor%d" % c, align_bytes=64)
             factor.append(tile)
             for t in range(PACK):
-                nc.scalar.activation(tile[:, t, :], spread[:, c * CHUNK : (c + 1) * CHUNK], COPY, scale=cs[:, t : t + 1])
+                nc.scalar.activation(tile[:, t, :], spread[c][:], COPY, scale=cs[:, t : t + 1])
 
         def quantize_w(h, t):
             cols = slice(t * P + h * half_m, t * P + (h + 1) * half_m)
@@ -134,7 +139,7 @@ def tile_picked_tokscale_none_po_kernel(tc, x_words, x_scales, tscale, cscale, w
                 in_=w_bf[h][:, t * W_HALF : (t + 1) * W_HALF],
             )
 
-        xw_picked = keep.tile([P, S], U32, name="xw_picked", tag="w_raw1", align_bytes=64)
+        xw_picked = keep.tile([P, S], U32, name="xw_picked", align_bytes=64)
 
         def gather_words(s0, s1):
             nc.vector.tensor_copy(
@@ -142,12 +147,10 @@ def tile_picked_tokscale_none_po_kernel(tc, x_words, x_scales, tscale, cscale, w
                 xw_window[:].bitcast(U32).indirect(offsets[:, s0 // 16 : s1 // 16]),
             )
 
-        for t in range(PACK):
-            quantize_w(0, t)
-        quantize_w(1, 0)
+        for h in range(2):
+            for t in range(PACK):
+                quantize_w(h, t)
         gather_words(0, P)
-        for t in range(1, PACK):
-            quantize_w(1, t)
         gather_words(P, CHUNK)
         gather_words(CHUNK, S)
 
@@ -177,14 +180,15 @@ def tile_picked_tokscale_none_po_kernel(tc, x_words, x_scales, tscale, cscale, w
             banks = [(0, 2, 0, P), (2, PACK, 0, P), (0, PACK, P, CHUNK)] if c == 0 else [(0, PACK, 0, P), (0, PACK, P, CHUNK)]
             for b, (t0, t1, s0, s1) in enumerate(banks):
                 tokens = slice(c * CHUNK + s0, c * CHUNK + s1)
-                acc = psum.tile([P, t1 - t0, s1 - s0], F32, name="acc%d_%d" % (c, b))
+                bank = "turned0" if (c, b) == (1, 1) else "acc%d_%d" % (c, b)
+                acc = psum.tile([P, t1 - t0, s1 - s0], F32, name="acc%d_%d" % (c, b), tag=bank)
                 for t in range(t0, t1):
                     nc.tensor.matmul_mx(
                         out=acc[:, t - t0, :],
                         lhsT=w_codes[:, t * P : (t + 1) * P].bitcast(FP8X4),
                         lhsT_scale=w_scales[:, t * P : (t + 1) * P],
                         rhs=xw_picked[:, tokens].bitcast(FP8X4),
-                        rhs_scale=xs_picked[:, tokens],
+                        rhs_scale=xs_placed[:, tokens],
                         start=True,
                         stop=True,
                     )

@@ -23,6 +23,7 @@ PACK = 4
 W_HALF = N // 2
 CHUNK = 256
 SCALAR_LAST = 64
+SCALAR_EARLY = 40
 SCALAR_LATE = 48
 SCALE_ROW0 = P - 16
 LIVE = P - 1
@@ -117,8 +118,9 @@ def tile_picked_tokscale_none_po_kernel(tc, x_words, x_scales, tscale, cscale, w
                 w_raw[u][:, :, h * W_HALF : (h + 1) * W_HALF].rearrange("p j (m t) -> p m j t", t=PACK)[:, m0:m1],
             )
 
-        for h in range(2):
-            round_w(nc.vector.tensor_copy, 0, h, 0, half_m)
+        round_w(nc.vector.tensor_copy, 0, 0, 0, half_m)
+        round_w(nc.scalar.copy, 0, 1, 0, SCALAR_EARLY)
+        round_w(nc.vector.tensor_copy, 0, 1, SCALAR_EARLY, half_m)
         round_w(nc.vector.tensor_copy, 1, 0, 0, half_m)
         round_w(nc.scalar.copy, 1, 1, 0, SCALAR_LATE)
         round_w(nc.vector.tensor_copy, 1, 1, SCALAR_LATE, half_m)

@@ -26,6 +26,7 @@ SCALAR_LAST = 64
 SCALAR_EARLY = 40
 SCALAR_LATE = 48
 SCALE_ROW0 = P - 16
+DMA_ALIGN = 256
 LIVE = P - 1
 
 
@@ -38,23 +39,23 @@ def tile_picked_tokscale_none_po_kernel(tc, x_words, x_scales, tscale, cscale, w
         offsets = keep.tile([P, S // 16], U16, name="offsets")
         nc.sync.dma_start(offsets[:], offs)
 
-        ts_window = keep.tile([P, T], F32, name="ts_window", align_bytes=64)
+        ts_window = keep.tile([P, T], F32, name="ts_window", align_bytes=DMA_ALIGN)
         nc.scalar.dma_start(ts_window[LIVE : LIVE + 1, :], tscale[0:1, :])
 
-        xs_window = keep.tile([P, T], U8, name="xs_window", align_bytes=64)
+        xs_window = keep.tile([P, T], U8, name="xs_window", align_bytes=DMA_ALIGN)
         nc.sync.dma_start(xs_window[SCALE_ROW0:, :].bitcast(I32), x_scales[0].bitcast(I32))
 
         w_view = w1.rearrange("(p j) m -> p j m", j=PACK)
         w_raw = []
         for u in range(2):
-            raw = keep.tile([P, 2, N], F32, name="w_raw%d" % u, align_bytes=64)
+            raw = keep.tile([P, 2, N], F32, name="w_raw%d" % u, align_bytes=DMA_ALIGN)
             nc.sync.dma_start(raw[:], w_view[:, 2 * u : 2 * u + 2, :])
             w_raw.append(raw)
 
         cs = keep.tile([P, PACK], F32, name="cs")
         nc.sync.dma_start(cs[:], cscale.rearrange("(p t) o -> p (t o)", t=PACK))
 
-        xw_window = keep.tile([P, T], I32, name="xw_window", align_bytes=64)
+        xw_window = keep.tile([P, T], I32, name="xw_window", align_bytes=DMA_ALIGN)
         nc.sync.dma_start(xw_window[:], x_words[0].rearrange("p n t -> p (n t)").bitcast(I32))
 
         ones = keep.tile([P, P], F32, name="ones")
@@ -73,10 +74,10 @@ def tile_picked_tokscale_none_po_kernel(tc, x_words, x_scales, tscale, cscale, w
         off_diagonal = keep.tile([P, P], F32, name="off_diagonal")
         nc.vector.tensor_scalar(off_diagonal[:], column_count[:], quadrant_start[:], row_count[:, 0:1], SUBTRACT, NOT_EQUAL)
         nc.scalar.activation(ident[:], off_diagonal[:], COPY, scale=-1.0, bias=1.0)
-        xs_placed = keep.tile([P, S], U8, name="xs_placed", align_bytes=64)
+        xs_placed = keep.tile([P, S], U8, name="xs_placed", align_bytes=DMA_ALIGN)
         nc.vector.memset(xs_placed[:].bitcast(I32), 0)
 
-        xs_picked = keep.tile([P, S], U8, name="xs_picked", align_bytes=64)
+        xs_picked = keep.tile([P, S], U8, name="xs_picked", align_bytes=DMA_ALIGN)
         nc.vector.tensor_copy(xs_picked[:], xs_window[:].indirect(offsets[:]))
         for q in range(4):
             nc.sync.dma_start(
@@ -156,8 +157,8 @@ def tile_picked_tokscale_none_po_kernel(tc, x_words, x_scales, tscale, cscale, w
         gather_words(P, CHUNK)
         gather_words(CHUNK, S)
 
-        y_codes = keep.tile([P, S], I32, name="y_codes", align_bytes=64)
-        y_scales = keep.tile([P, S], U8, name="y_scales", align_bytes=64)
+        y_codes = keep.tile([P, S], I32, name="y_codes", align_bytes=DMA_ALIGN)
+        y_scales = keep.tile([P, S], U8, name="y_scales", align_bytes=DMA_ALIGN)
         y_bf = keep.tile([P, S * PACK], BF16, name="y_bf", align_bytes=64)
         out_rows = out_0.rearrange("(p t) s -> p t s", t=PACK)
         out_words = out_1[0].rearrange("p s t -> p (s t)").bitcast(I32)
@@ -177,7 +178,7 @@ def tile_picked_tokscale_none_po_kernel(tc, x_words, x_scales, tscale, cscale, w
             )
 
         for c in range(n_chunks):
-            tile = keep.tile([P, PACK, CHUNK], F32, name="y%d" % c, align_bytes=64)
+            tile = keep.tile([P, PACK, CHUNK], F32, name="y%d" % c, align_bytes=DMA_ALIGN)
             y.append(tile)
             banks = [(0, 2, 0, P), (2, PACK, 0, P), (0, PACK, P, CHUNK)] if c == 0 else [(0, PACK, 0, P), (0, PACK, P, CHUNK)]
             for b, (t0, t1, s0, s1) in enumerate(banks):

@@ -23,8 +23,7 @@ PACK = 4
 W_HALF = N // 2
 CHUNK = 256
 SCALAR_LAST = 64
-SCALAR_EARLY = 40
-SCALAR_LATE = 48
+SCALAR_LATE = 40
 SCALE_ROW0 = P - 16
 DMA_ALIGN = 256
 LIVE = P - 1
@@ -108,23 +107,17 @@ def tile_picked_tokscale_none_po_kernel(tc, x_words, x_scales, tscale, cscale, w
         w_codes = keep.tile([P, N], U32, name="w_codes", align_bytes=64)
         w_scales = keep.tile([P, N], U8, name="w_scales", align_bytes=64)
         half_m = W_HALF // PACK
-        w_bf = []
-        for h in range(2):
-            bf = keep.tile([P, W_HALF * PACK], BF16, name="w_bf%d" % h, align_bytes=64)
-            w_bf.append(bf)
+        w_bf = keep.tile([P, 2, PACK, half_m, PACK], BF16, name="w_bf", align_bytes=64)
+        w_pairs = w_bf[:].rearrange("p h t m (u j) -> p u h m j t", u=2)
 
-        def round_w(copy, u, h, m0, m1):
-            copy(
-                w_bf[h][:].rearrange("p (t m u j) -> p u m j t", t=PACK, u=2, j=2)[:, u, m0:m1],
-                w_raw[u][:, :, h * W_HALF : (h + 1) * W_HALF].rearrange("p j (m t) -> p m j t", t=PACK)[:, m0:m1],
-            )
+        def raw_pair(u):
+            return w_raw[u][:].rearrange("p j (h m t) -> p h m j t", h=2, t=PACK)
 
-        round_w(nc.vector.tensor_copy, 0, 0, 0, half_m)
-        round_w(nc.scalar.copy, 0, 1, 0, SCALAR_EARLY)
-        round_w(nc.vector.tensor_copy, 0, 1, SCALAR_EARLY, half_m)
-        round_w(nc.vector.tensor_copy, 1, 0, 0, half_m)
-        round_w(nc.scalar.copy, 1, 1, 0, SCALAR_LATE)
-        round_w(nc.vector.tensor_copy, 1, 1, SCALAR_LATE, half_m)
+        nc.vector.tensor_copy(w_pairs[:, 0], raw_pair(0))
+        for t0 in range(0, PACK, 2):
+            nc.vector.tensor_copy(w_pairs[:, 1, 0, :, :, t0 : t0 + 2], raw_pair(1)[:, 0, :, :, t0 : t0 + 2])
+        nc.scalar.copy(w_pairs[:, 1, 1, :SCALAR_LATE], raw_pair(1)[:, 1, :SCALAR_LATE])
+        nc.vector.tensor_copy(w_pairs[:, 1, 1, SCALAR_LATE:], raw_pair(1)[:, 1, SCALAR_LATE:])
 
         n_chunks = S // CHUNK
         factor = []
@@ -139,7 +132,7 @@ def tile_picked_tokscale_none_po_kernel(tc, x_words, x_scales, tscale, cscale, w
             nc.vector.quantize_mx(
                 out=w_codes[:, cols].bitcast(FP8X4),
                 scales=w_scales[:, cols],
-                in_=w_bf[h][:, t * W_HALF : (t + 1) * W_HALF],
+                in_=w_bf[:, h, t].rearrange("p m j -> p (m j)"),
             )
 
         xw_picked = keep.tile([P, S], U32, name="xw_picked", align_bytes=64)

from contextlib import ExitStack

import concourse.mybir as mybir

K, T, S, N = 512, 1024, 512, 512
FLOPS = 2 * K * S * N

F32 = mybir.dt.float32
BF16 = mybir.dt.bfloat16
I32 = mybir.dt.int32
U32 = mybir.dt.uint32
U16 = mybir.dt.uint16
U8 = mybir.dt.uint8
FP8X4 = mybir.dt.float8_e4m3fn_x4
MULT = mybir.AluOpType.mult
ADD = mybir.AluOpType.add
SUBTRACT = mybir.AluOpType.subtract
NOT_EQUAL = mybir.AluOpType.not_equal
COPY = mybir.ActivationFunctionType.Copy

P = 128
PACK = 4
W_HALF = N // 2
CHUNK = 256
SCALAR_LAST = 64
SCALAR_LATE = 40
SCALE_ROW0 = P - 16
DMA_ALIGN = 256
LIVE = P - 1


def tile_picked_tokscale_none_po_kernel(tc, x_words, x_scales, tscale, cscale, w1, offs, out_0, out_1, out_2):
    nc = tc.nc
    with ExitStack() as ctx:
        keep = ctx.enter_context(tc.tile_pool(name="keep", bufs=1))
        psum = ctx.enter_context(tc.psum_pool(name="psum", bufs=1))

        offsets = keep.tile([P, S // 16], U16, name="offsets")
        nc.sync.dma_start(offsets[:], offs)

        ts_window = keep.tile([P, T], F32, name="ts_window", align_bytes=DMA_ALIGN)
        nc.scalar.dma_start(ts_window[LIVE : LIVE + 1, :], tscale[0:1, :])

        xs_window = keep.tile([P, T], U8, name="xs_window", align_bytes=DMA_ALIGN)
        nc.sync.dma_start(xs_window[SCALE_ROW0:, :].bitcast(I32), x_scales[0].bitcast(I32))

        w_view = w1.rearrange("(p j) m -> p j m", j=PACK)
        w_raw = []
        for u in range(2):
            raw = keep.tile([P, 2, N], F32, name="w_raw%d" % u, align_bytes=DMA_ALIGN)
            nc.sync.dma_start(raw[:], w_view[:, 2 * u : 2 * u + 2, :])
            w_raw.append(raw)

        cs = keep.tile([P, PACK], F32, name="cs")
        nc.sync.dma_start(cs[:], cscale.rearrange("(p t) o -> p (t o)", t=PACK))

        xw_window = keep.tile([P, T], I32, name="xw_window", align_bytes=DMA_ALIGN)
        nc.sync.dma_start(xw_window[:], x_words[0].rearrange("p n t -> p (n t)").bitcast(I32))

        ones = keep.tile([P, P], F32, name="ones")
        nc.gpsimd.memset(ones[:], 1.0)
        quadrant_start = keep.tile([P, 1], F32, name="quadrant_start")
        for q in range(4):
            nc.gpsimd.memset(quadrant_start[32 * q : 32 * q + 32, :], 32.0 * q)
        nc.vector.memset(xs_window[0:SCALE_ROW0, :].bitcast(I32), 0)
        column_count = keep.tile([P, P], F32, name="column_count", align_bytes=64)
        nc.vector.tensor_tensor_scan(column_count[:], ones[:], ones[:], 0.0, MULT, ADD)
        nc.vector.memset(ts_window[0:LIVE, : T // 2], 0.0)
        row_count = keep.tile([P, 32], F32, name="row_count", align_bytes=64)
        nc.vector.transpose(row_count[:], column_count[:, 0:32])
        nc.vector.memset(ts_window[0:LIVE, T // 2 :], 0.0)
        ident = keep.tile([P, P], F32, name="ident")
        off_diagonal = keep.tile([P, P], F32, name="off_diagonal")
        nc.vector.tensor_scalar(off_diagonal[:], column_count[:], quadrant_start[:], row_count[:, 0:1], SUBTRACT, NOT_EQUAL)
        nc.scalar.activation(ident[:], off_diagonal[:], COPY, scale=-1.0, bias=1.0)
        xs_placed = keep.tile([P, S], U8, name="xs_placed", align_bytes=DMA_ALIGN)
        nc.vector.memset(xs_placed[:].bitcast(I32), 0)

        xs_picked = keep.tile([P, S], U8, name="xs_picked", align_bytes=DMA_ALIGN)
        nc.vector.tensor_copy(xs_picked[:], xs_window[:].indirect(offsets[:]))
        for q in range(4):
            nc.sync.dma_start(
                xs_placed[32 * q : 32 * q + 4, :].bitcast(I32),
                xs_picked[SCALE_ROW0 + 4 * q : SCALE_ROW0 + 4 * q + 4, :].bitcast(I32),
            )

        ts_row = keep.tile([P, S], F32, name="ts_row", align_bytes=64)
        for h in range(2):
            nc.scalar.activation(
                ts_row[:, h * CHUNK : (h + 1) * CHUNK],
                ts_window[:].indirect(offsets[:, h * CHUNK // 16 : (h + 1) * CHUNK // 16]),
                COPY,
            )

        spread = []
        for h in range(2):
            turned = psum.tile([P, 2, P], F32, name="turned%d" % h, tag="turned%d" % h)
            for b in range(2):
                nc.tensor.transpose(turned[:, b, :], ts_row[:, (2 * h + b) * P : (2 * h + b + 1) * P], ident[:])
            ts_cols = keep.tile([P, 2], F32, name="ts_cols%d" % h, align_bytes=64)
            nc.scalar.copy(ts_cols[:], turned[:, :, LIVE])
            bank = psum.tile([P, CHUNK], F32, name="spread%d" % h)
            spread.append(bank)
            for b in range(2):
                nc.tensor.transpose(bank[:, b * P : (b + 1) * P], ts_cols[:, b : b + 1].to_broadcast([P, P]), ident[:])

        w_codes = keep.tile([P, N], U32, name="w_codes", align_bytes=64)
        w_scales = keep.tile([P, N], U8, name="w_scales", align_bytes=64)
        half_m = W_HALF // PACK
        w_bf = keep.tile([P, 2, PACK, half_m, PACK], BF16, name="w_bf", align_bytes=64)
        w_pairs = w_bf[:].rearrange("p h t m (u j) -> p u h m j t", u=2)

        def raw_pair(u):
            return w_raw[u][:].rearrange("p j (h m t) -> p h m j t", h=2, t=PACK)

        nc.vector.tensor_copy(w_pairs[:, 0], raw_pair(0))
        for t0 in range(0, PACK, 2):
            nc.vector.tensor_copy(w_pairs[:, 1, 0, :, :, t0 : t0 + 2], raw_pair(1)[:, 0, :, :, t0 : t0 + 2])
        nc.scalar.copy(w_pairs[:, 1, 1, :SCALAR_LATE], raw_pair(1)[:, 1, :SCALAR_LATE])
        nc.vector.tensor_copy(w_pairs[:, 1, 1, SCALAR_LATE:], raw_pair(1)[:, 1, SCALAR_LATE:])

        n_chunks = S // CHUNK
        factor = []
        for c in range(n_chunks):
            tile = keep.tile([P, PACK, CHUNK], F32, name="factor%d" % c, align_bytes=64)
            factor.append(tile)
            for t in range(PACK):
                nc.scalar.activation(tile[:, t, :], spread[c][:], COPY, scale=cs[:, t : t + 1])

        def quantize_w(h, t):
            cols = slice(t * P + h * half_m, t * P + (h + 1) * half_m)
            nc.vector.quantize_mx(
                out=w_codes[:, cols].bitcast(FP8X4),
                scales=w_scales[:, cols],
                in_=w_bf[:, h, t].rearrange("p m j -> p (m j)"),
            )

        xw_picked = keep.tile([P, S], U32, name="xw_picked", align_bytes=64)

        def gather_words(s0, s1):
            nc.vector.tensor_copy(
                xw_picked[:, s0:s1],
                xw_window[:].bitcast(U32).indirect(offsets[:, s0 // 16 : s1 // 16]),
            )

        for h in range(2):
            for t in range(PACK):
                quantize_w(h, t)
        gather_words(0, P)
        gather_words(P, CHUNK)
        gather_words(CHUNK, S)

        y_codes = keep.tile([P, S], I32, name="y_codes", align_bytes=DMA_ALIGN)
        y_scales = keep.tile([P, S], U8, name="y_scales", align_bytes=DMA_ALIGN)
        y_bf = keep.tile([P, S * PACK], BF16, name="y_bf", align_bytes=64)
        out_rows = out_0.rearrange("(p t) s -> p t s", t=PACK)
        out_words = out_1[0].rearrange("p s t -> p (s t)").bitcast(I32)
        y = []

        def round_y(copy, c, s0, s1):
            copy(
                y_bf[:, (c * CHUNK + s0) * PACK : (c * CHUNK + s1) * PACK].rearrange("p (g i t) -> p g t i", i=4, t=PACK),
                y[c][:, :, s0:s1].rearrange("p t (g i) -> p g t i", i=4),
            )

        def quantize_y(s0, s1):
            nc.vector.quantize_mx(
                out=y_codes[:, s0:s1].bitcast(FP8X4),
                scales=y_scales[:, s0:s1],
                in_=y_bf[:, s0 * PACK : s1 * PACK],
            )

        for c in range(n_chunks):
            tile = keep.tile([P, PACK, CHUNK], F32, name="y%d" % c, align_bytes=DMA_ALIGN)
            y.append(tile)
            banks = [(0, 2, 0, P), (2, PACK, 0, P), (0, PACK, P, CHUNK)] if c == 0 else [(0, PACK, 0, P), (0, PACK, P, CHUNK)]
            for b, (t0, t1, s0, s1) in enumerate(banks):
                tokens = slice(c * CHUNK + s0, c * CHUNK + s1)
                bank = "turned0" if (c, b) == (1, 1) else "acc%d_%d" % (c, b)
                acc = psum.tile([P, t1 - t0, s1 - s0], F32, name="acc%d_%d" % (c, b), tag=bank)
                for t in range(t0, t1):
                    nc.tensor.matmul_mx(
                        out=acc[:, t - t0, :],
                        lhsT=w_codes[:, t * P : (t + 1) * P].bitcast(FP8X4),
                        lhsT_scale=w_scales[:, t * P : (t + 1) * P],
                        rhs=xw_picked[:, tokens].bitcast(FP8X4),
                        rhs_scale=xs_placed[:, tokens],
                        start=True,
                        stop=True,
                    )
                nc.vector.tensor_tensor(tile[:, t0:t1, s0:s1], acc[:], factor[c][:, t0:t1, s0:s1], MULT)
                nc.sync.dma_start(out_rows[:, t0:t1, tokens], tile[:, t0:t1, s0:s1])
                if t1 == PACK:
                    round_y(nc.scalar.copy, c, s0, s1 if (c, s0) != (1, P) else P + SCALAR_LAST)

        quantize_y(0, CHUNK)
        nc.sync.dma_start(out_words[:, :CHUNK], y_codes[:, :CHUNK])
        round_y(nc.vector.tensor_copy, 1, P + SCALAR_LAST, CHUNK)
        quantize_y(CHUNK, CHUNK + P)
        quantize_y(CHUNK + P, S)
        nc.sync.dma_start(out_words[:, CHUNK:], y_codes[:, CHUNK:])

        for q in range(4):
            engine = nc.sync if q == 0 else nc.scalar
            engine.dma_start(
                out_2[0, 4 * q : 4 * q + 4, :].bitcast(I32),
                y_scales[32 * q : 32 * q + 4, :].bitcast(I32),
            )
